import numpy as np, ml_dtypes
CORES = [16,18,20,22]
N = 4
import mx_ref
BF = ml_dtypes.bfloat16
def pick(q, e):
    c = np.concatenate([q[0].reshape(128, -1, 4), np.zeros((128, 1, 4), np.uint8)], axis=1); s = np.concatenate([q[1], np.ones((16, 1), np.uint8)], axis=1)
    return (np.ascontiguousarray(c[:, e].reshape(128, -1)), np.ascontiguousarray(s[:, e]))
def join(*qs):
    return (np.concatenate([q[0] for q in qs], axis=1), np.concatenate([q[1] for q in qs], axis=1))
def put(q, e, v):
    c, s = q[0].reshape(128, -1, 4).copy(), q[1].copy(); c[:, e] = v[0].reshape(128, -1, 4); s[:, e] = v[1]
    return (c.reshape(128, -1), s)
def pk(c, s):
    return (np.ascontiguousarray(c), mx_ref.live(s))
def emit(q):
    return q[0], q[1]
def decode(q):
    o = []
    for b in range(4):
        e = np.zeros((128, 128, 4), np.float32); e[np.arange(128), np.arange(128), b] = 1
        o.append(mx_ref.matmul(mx_ref.quantize(e.reshape(128, 512).astype(BF)), q))
    return np.stack(o, axis=2).reshape(128, -1)
def cols(t, e):
    v = np.concatenate([t.reshape(128, -1, 4), np.zeros((128, 1, 4), BF)], axis=1)
    return np.ascontiguousarray(v[:, e]).reshape(128, -1)
def cut(t, i, w=512):
    return t[:, w * i:w * i + w]
def f(rng, *shape):
    return mx_ref.flush((rng.standard_normal(shape, dtype=np.float32) * np.exp2(rng.integers(-2, 3, shape[:-1] + (1,)))).astype(BF))
def wide(rng, *shape, cols=0):
    v = rng.standard_normal(shape, dtype=np.float32) * np.exp2(rng.integers(-12, 13, shape)).astype(np.float32)
    if cols: v *= np.repeat(np.exp2(rng.integers(-cols, cols + 1, shape[:-2] + (1, shape[-1] // 4))) * (rng.random(shape[:-2] + (1, shape[-1] // 4)) > 0.0625), 4, axis=-1).astype(np.float32)
    return mx_ref.flush(v.astype(BF))
C, T, R, O = 384, 96, 2, 1
def trim(v):
    v = v.astype(np.float32)
    v[np.abs(v) < np.float32(2.0 ** -14)] = 0
    return v.astype(BF)
def given(rng, u, x):
    return {"kb": np.stack([trim(u.reshape(128, 4 * C))] * N), "x": trim(x.reshape(N, 128, 4 * R * T)), "w": f(rng, N, 128, 512 * O)}
def sturdy(rng, n):
    return (1 + rng.random((128, n, 4))) * rng.choice([-1.0, 1.0], (128, n, 4)) * np.exp2(rng.integers(-1, 2, (128, 1, 1)))
def kept(v):
    m, e = np.frexp(v)
    return np.ldexp(np.trunc(m * 8) * 0.125, e)
def near(rng, u, e):
    return u[:, e] + 0.5 * sturdy(rng, len(e))
def setup_inputs(rng):
    return given(rng, f(rng, 128, 4 * C), f(rng, N, 128, 4 * R * T))
def setup_inputs_both(rng):
    u, x, new = kept(sturdy(rng, C)), np.zeros((N, 128, R, T, 4)), np.zeros((N, C), bool)
    for b in range(R):
        for j, r in enumerate(rng.permutation([v for v in range(N) if v < v ^ (1 << b)])):
            p, e = r ^ (1 << b), rng.permutation(C)
            if j % 2: e = e[np.argsort(new[r, e] | ~new[p, e], kind="stable")]
            t = e[T:2 * T] if j % 2 else rng.permutation(e[:T])
            x[r, :, b] = near(rng, u, e[:T])
            x[r, :, b, :T // 4] = u[:, e[:T // 4]]
            x[p, :, b] = near(rng, u, t)
            for s in (r, p):
                new[s, e[:T]] = True
                new[s, t] = True
    return given(rng, u, x)
def setup_inputs_few(rng):
    u, x, four = sturdy(rng, C), np.zeros((N, 128, R, T, 4)), rng.permutation(C)[:4]
    for b in range(R):
        for j, r in enumerate(rng.permutation([v for v in range(N) if v < v ^ (1 << b)])):
            a = rng.permutation(four)[:2]
            for s, c in ((r, a[0]), (r ^ (1 << b), a[j % 2])):
                x[s, :, b] = near(rng, u, np.full(T, c)) * np.exp2(rng.integers(-1, 2, (1, T, 1)))
    return given(rng, u, x)
def setup_inputs_ties(rng):
    u = np.abs(cols(f(rng, 128, 4 * (C // 4)), rng.permutation(np.arange(C) % (C // 4))).astype(np.float32))
    x = np.abs(f(rng, N, 128, 4 * R * T).astype(np.float32)).reshape(N, 128, R, T, 4)
    for r in range(N):
        for b in range(R):
            x[r, :, b] *= (1 - 2 * (rng.permutation(T) % 2)).astype(np.float32)[:, None]
            x[r, :, b, int(rng.integers(0, T))] = 0
    return given(rng, u * np.float32(2.0 ** 18), x * np.float32(2.0 ** 18))
def setup_inputs_drift(rng):
    top = (rng.permutation(128) < 64)[:, None, None]
    u, z, x = sturdy(rng, C) * top, sturdy(rng, 8) * ~top, np.zeros((N, 128, R, T, 4))
    e = rng.permutation(C)
    for r in range(N):
        for b in range(R):
            t = rng.permutation(e[:C // 2] if b == 0 else e[C // 2:])[:T]
            x[r, :, b] = near(rng, u, t) * top + 8 * z[:, rng.permutation(np.arange(T) % 8)]
    return given(rng, u, x)
def setup_inputs_spread(rng):
    d = given(rng, wide(rng, 128, 4 * C, cols=2), wide(rng, N, 128, 4 * R * T, cols=6))
    d["kb"][:, :, :4] = BF(-0.0)
    for r in range(N):
        for b in range(R):
            i = 4 * (b * T + int(rng.integers(0, T)))
            d["x"][r, :, i:i + 4] = BF(0.0)
    return d
def check_inputs(d):
    b = []
    for n, lo, hi in (("kb", -14, 24), ("x", -14, 24), ("w", -30, 30)):
        v = np.abs(d[n].astype(np.float32))
        if not (np.isfinite(v).all() and ((v == 0) | (v >= 2.0 ** lo) & (v <= 2.0 ** hi)).all()): b.append("a value of " + n)
    if (d["kb"].astype(np.float32) != d["kb"][:1].astype(np.float32)).any(): b.append("kb isn't the same on all ranks")
    return b
def numbers(k, e):
    return decode(pick(k, np.concatenate([e, np.full(-len(e) % 4, -1)]))).reshape(128, -1, 4)[:, :len(e)]
def anew(k, e, v):
    t = np.zeros((128, len(e) + -len(e) % 4, 4), np.float32)
    t[:, :len(e)] = v
    return put(k, e, pick(mx_ref.quantize(t.reshape(128, -1).astype(BF)), np.arange(len(e))))
def reference(kb, x, w):
    k = join(*[mx_ref.quantize(np.ascontiguousarray(kb[r])) for r in range(N)])
    q = join(*[mx_ref.quantize(np.ascontiguousarray(x[r])) for r in range(N)])
    dx = decode(q).reshape(128, N, R, T, 4)
    ch = np.zeros((N, R, T), np.float32)
    for b in range(R):
        won, e, t = np.zeros((N, C), bool), [], []
        for r in range(N):
            v = pick(q, (r * R + b) * T + np.arange(T))
            s = np.concatenate([mx_ref.matmul(pick(k, C * r + 128 * m + np.arange(128)), v) for m in range(C // 128)])
            win = np.argmax(s + np.float32(0), axis=0)
            u, i = np.unique(win, return_index=True)
            won[r, u] = True
            e.append(C * r + u)
            t.append(dx[:, r, b, i])
            ch[r, b] = win
        e = np.concatenate(e)
        k = anew(k, e, np.float32(0.75) * numbers(k, e) + np.float32(0.25) * np.concatenate(t, axis=1))
        src, low, high = np.arange(N * C).reshape(N, C), [], []
        for r in range(N):
            p = r ^ (1 << b)
            src[r] = np.where(won[p] & ~won[r], C * p + np.arange(C), src[r])
            if r < p:
                u = np.flatnonzero(won[r] & won[p])
                low.append(C * r + u)
                high.append(C * p + u)
        low, high = np.concatenate(low), np.concatenate(high)
        if len(low):
            v = np.float32(0.5) * numbers(k, low) + np.float32(0.5) * numbers(k, high)
            k = anew(k, np.concatenate([low, high]), np.concatenate([v, v], axis=1))
        k = pick(k, src.reshape(-1))
    oc, osc, y = np.zeros((N, 128, 4 * C), np.uint8), np.zeros((N, 16, C), np.uint8), np.zeros((N, 128, O * C), np.float32)
    for r in range(N):
        t = pick(k, C * r + np.arange(C))
        oc[r], osc[r] = emit(t)
        for o in range(O): y[r, :, C * o:C * o + C] = mx_ref.matmul(mx_ref.quantize(np.ascontiguousarray(cut(w[r], o))), t)
    return {"oc": oc, "osc": osc, "ch": ch, "y": y}

@@ -1,0 +1,446 @@
+from concourse.mybir import dt, AluOpType, AxisListType, ActivationFunctionType
+
+A = AluOpType
+AF = ActivationFunctionType
+NU, NT, NR = 384, 96, 2
+OWN, PAR, MRG, WIN = 384, 512, 640, 736
+MQ = 608
+XC, XL = 128, 102
+F4, F32, BF, U16, I32, U8 = "float8_e4m3fn_x4", "float32", "bfloat16", "uint16", "int32", "uint8"
+
+
+def _decl():
+    s = {}
+
+    def add(n, w, t, where="sbuf"):
+        s[n] = (where, [128, w], t)
+
+    def pair(n, w):
+        add(n, w, F4)
+        add(n + "s", w, U8)
+    for b in range(NR):
+        pair("tab%d" % b, WIN)
+        pair("xq%d" % b, 128)
+        add("xt%d" % b, 512, BF)
+        for n in ("lown", "land", "lx", "lxp"):
+            add("%s%d" % (n, b), 6, U16)
+        add("mslot%d" % b, 480, F32)
+        add("src%d" % b, 480, F32)
+        add("win%d" % b, 1, F32)
+    for n in ("e25", "e75", "e50"):
+        pair(n, 512)
+        add("z" + n, 520, BF)
+    for n in ("r16", "r1", "negw"):
+        pair(n, 128)
+        add("t" + n, 512, BF)
+    for n in ("sel", "selm", "xl", "xf", "wq"):
+        pair(n, 128)
+    pair("fin", NU)
+    for n in range(8):
+        add("ps%d" % n, 512, F32, "psum")
+    for n, w, t in (("kbt", 1536, BF), ("wt", 512, BF), ("nt", 512, BF), ("mt", 512, BF), ("xtile", 4 * XC, BF), ("ftile", 512, BF),
+                    ("fsend", 4, BF), ("fland", 4, BF), ("z1", 520, BF), ("mask", XL, BF), ("mask36", 36, BF), ("eq16", 128, BF),
+                    ("junk", NU, BF), ("mb", XL, BF), ("mbh", XL, BF), ("ip", 1, I32), ("pmi", 1, I32), ("pdi", 1, I32),
+                    ("clist", 6, U16), ("blist", 24, U16)):
+        add(n, w, t)
+    for n, w in (("iotac", 520), ("cmod", NU), ("jown", NT), ("jpar", NT), ("t6", 6), ("t6s", 6), ("pcol", 1), ("p4", 1), ("pm", 1),
+                 ("pd", 1), ("negc", 128), ("diagm", NU), ("reset", NU), ("p", NU), ("zz", 24), ("h1", 1), ("h2", 1), ("dmin", 1),
+                 ("d6", 6), ("tx", 6), ("tx2", 6), ("mval", NT), ("mf1", NU), ("mflag", NU), ("c1", NT), ("c2", NT), ("val", NT),
+                 ("pval", NT), ("lpf", 6), ("d6p", 6), ("fb", 6), ("txp", 6), ("txp2", 6), ("srcs", NU), ("ysb", NU)):
+        add(n, w, F32)
+    return s
+
+
+SCRATCH = _decl()
+NCOMP, NHW = 90, 30
+REMOTE = ["%s%d" % (n, b) for b in range(NR) for n in ("al", "ac", "af")] + ["ll", "lc", "lf"]
+SEMAPHORES = ["c%d" % i for i in range(NCOMP)] + ["h%d" % i for i in range(NHW)] + REMOTE
+
+
+def _clash(u, v):
+    if u[1] >= v[2] or v[1] >= u[2]:
+        return False
+    return not (u[3] == v[3] and u[3] > 1 and (u[1] - v[1]) % u[3])
+
+
+def _record(rec, queue, kind, call, reads, writes, extra=()):
+    ops, acc = rec["ops"], rec["acc"]
+    i = len(ops)
+    deps = set(extra)
+    for vs, w in ((reads, False), (writes, True)):
+        for v in vs:
+            for (u, uw, j, uq) in acc.get(v[0], []):
+                if v[0] in rec["psum"]:
+                    if uq == "tensor" and queue == "tensor":
+                        continue
+                    if uq != queue or uw:
+                        deps.add(j)
+                elif (w or uw) and _clash(u, v):
+                    deps.add(j)
+    for vs, w in ((reads, False), (writes, True)):
+        for v in vs:
+            acc.setdefault(v[0], []).append((v, w, i, queue))
+    if kind == "arr" and deps:
+        raise ValueError("a landing buffer is in use")
+    known = rec["known"].setdefault(queue, set()) if kind != "arr" else set()
+    waits = []
+    for j in sorted(deps, reverse=True):
+        if j not in known:
+            waits.append(j)
+            known.add(j)
+            known |= ops[j]["known"]
+    ops.append({"queue": queue, "kind": kind, "call": call, "waits": waits, "known": set(known), "need": False})
+    for j in waits:
+        ops[j]["need"] = True
+    return i
+
+
+def _issue(rec, queues, sems):
+    ops = rec["ops"]
+    last, total = {}, {}
+    for i, o in enumerate(ops):
+        if o["kind"] == "arr":
+            o["sem"], o["val"] = o["call"]
+            continue
+        q = queues[o["queue"]]
+        for j in reversed(o["waits"]):
+            q.wait_ge(sems[ops[j]["sem"]], ops[j]["val"])
+        if o["kind"] == "end":
+            continue
+        ins = o["call"](q)
+        if not o["need"] or o["kind"] == "remote":
+            continue
+        pool = ["h%d" % k for k in range(NHW)] if o["kind"] == "dma" else ["c%d" % k for k in range(NCOMP)]
+        name = None
+        for s in pool:
+            if s not in last or last[s] in o["known"]:
+                name = s
+                break
+        if name is None:
+            raise ValueError("out of semaphores")
+        n = 16 if o["kind"] == "dma" else 1
+        ins.then_inc(sems[name], n)
+        last[name] = i
+        total[name] = total.get(name, 0) + n
+        o["sem"], o["val"] = name, total[name]
+
+
+def V(name, a, b, s=1):
+    return (name, a, b, s)
+
+
+def rank_program(g, core, T, topo):
+    rank = T.rank_of(core)
+    if rank is None:
+        return
+    rec = {"ops": [], "acc": {}, "known": {}, "psum": ["ps%d" % n for n in range(8)]}
+
+    def ap(v):
+        return T[v[0]][:, v[1]:v[2]] if v[3] == 1 else T[v[0]][:, v[1]:v[2]:v[3]]
+
+    def sc(v):
+        return (v[0] + "s", v[1], v[2], 1)
+
+    def views(*xs):
+        return [x for x in xs if isinstance(x, tuple)]
+
+    def val(x):
+        return ap(x) if isinstance(x, tuple) else x
+
+    def memset(out, c):
+        _record(rec, "vector", "comp", lambda q: q.memset(ap(out), c), [], [out])
+
+    def copy(out, in_, queue="vector", scale=None, bias=None, func=None):
+        if queue == "vector":
+            _record(rec, "vector", "comp", lambda q: q.tensor_copy(ap(out), ap(in_)), [in_], [out])
+            return
+        f = func or (AF.Copy if bias is None else AF.Identity)
+        kw = {}
+        if scale is not None:
+            kw["scale"] = scale
+        if bias is not None:
+            kw["bias"] = bias
+        _record(rec, "scalar", "comp", lambda q: q.activation(ap(out), ap(in_), f, **kw), [in_], [out])
+
+    def ts(out, in0, s1, op0, s2=None, op1=None):
+        def call(q):
+            if op1 is None:
+                return q.tensor_scalar(ap(out), ap(in0), val(s1), None, op0)
+            return q.tensor_scalar(ap(out), ap(in0), val(s1), val(s2), op0, op1)
+        _record(rec, "vector", "comp", call, views(in0, s1, s2), [out])
+
+    def tt(out, in0, in1, op, off=None):
+        def call(q):
+            i0 = ap(in0) if off is None else ap(in0).indirect(ap(off))
+            return q.tensor_tensor(ap(out), i0, ap(in1), op)
+        _record(rec, "vector", "comp", call, views(in0, in1, off), [out])
+
+    def scatter(win, off, in_):
+        _record(rec, "vector", "comp", lambda q: q.tensor_copy(ap(win).indirect(ap(off)), ap(in_)), [win, off, in_], [win])
+
+    def reduce(out, in_, op, absv=False):
+        def call(q):
+            if absv:
+                return q.tensor_reduce(ap(out), ap(in_), AxisListType.X, op, apply_absolute_value=True)
+            return q.tensor_reduce(ap(out), ap(in_), AxisListType.X, op)
+        _record(rec, "vector", "comp", call, [in_], [out])
+
+    def scan(out, d0, d1, init, op0, op1):
+        _record(rec, "vector", "comp", lambda q: q.tensor_tensor_scan(ap(out), ap(d0), ap(d1), val(init), op0, op1),
+                views(d0, d1, init), [out])
+
+    def quant(out, in_):
+        _record(rec, "vector", "comp", lambda q: q.quantize_mx(ap(out), ap(sc(out)), ap(in_)), [in_], [out, sc(out)])
+
+    def mm(ps, w, x, start=True, stop=True):
+        n = x[2] - x[1]
+        _record(rec, "tensor", "comp",
+                lambda q: q.matmul_mx(T["ps%d" % ps][:, 0:n], ap(w), ap(sc(w)), ap(x), ap(sc(x)), start, stop),
+                [w, sc(w), x, sc(x)], [V("ps%d" % ps, 0, n)])
+
+    def pick(out, win, off):
+        _record(rec, "vector", "comp",
+                lambda q: q.tensor_copy(ap(out).bitcast(dt.uint32), ap(win).bitcast(dt.uint32).indirect(ap(off))), [win, off], [out])
+        _record(rec, "scalar", "comp", lambda q: q.activation(ap(sc(out)), ap(sc(win)).indirect(ap(off)), AF.Copy),
+                [sc(win), off], [sc(out)])
+
+    def iota(out, pattern, base, cm):
+        f = SCRATCH[out[0]][2] != I32
+
+        def call(q):
+            if f:
+                return q.iota(ap(out), pattern, base, cm, allow_small_or_imprecise_dtypes=True)
+            return q.iota(ap(out), pattern, base, cm)
+        _record(rec, "gpsimd", "comp", call, [], [out])
+
+    def load(queue, out, src):
+        _record(rec, queue, "dma", lambda q: q.dma_start(ap(out), src), [], [out])
+
+    def lay(out, in_):
+        _record(rec, "sync", "dma", lambda q: q.dma_start(ap(out).bitcast(dt.uint8), ap(in_).bitcast(dt.uint8)), [in_], [out])
+        _record(rec, "sync", "dma", lambda q: q.dma_start(ap(sc(out)), ap(sc(in_))), [sc(in_)], [sc(out)])
+
+    stores = []
+
+    def store(queue, dst, in_, view):
+        stores.append(_record(rec, queue, "dma", lambda q: q.dma_start(dst, view), [in_], []))
+
+    def send(dst, out, in_, arr, loc):
+        rid, pid, _s = topo.addr(dst)
+        codes = SCRATCH[in_[0]][2] == F4
+
+        def call(q):
+            o, i = ap(out), ap(in_)
+            if codes:
+                o, i = o.bitcast(dt.uint8), i.bitcast(dt.uint8)
+            return q.remote_dma(o, i, T.sem[arr], T.sem[loc], pid, rid, topo.mask(core, dst))
+        _record(rec, "gpsimd", "remote", call, [in_], [])
+
+    def arrive(writes, sem, src, calls=1):
+        _record(rec, "network", "arr", (sem, calls * len(topo.engines(src, core))), [], writes)
+
+    load("sync", V("xt0", 0, 384), T.x[:, 0:384])
+    load("scalar", V("kbt", 0, 512), T.kb[:, 0:512])
+    load("sync", V("kbt", 512, 1024), T.kb[:, 512:1024])
+    load("scalar", V("kbt", 1024, 1536), T.kb[:, 1024:1536])
+    load("sync", V("xt1", 0, 384), T.x[:, 384:768])
+    load("sync", V("wt", 0, 512), T.w[:, 0:512])
+
+    iota(V("p4", 0, 1), [[0, 1]], 4, 4)
+    iota(V("ip", 0, 1), [[0, 1]], 0, 1)
+    iota(V("iotac", 0, 520), [[1, 520]], 0, 0)
+    iota(V("pcol", 0, 1), [[0, 1]], 0, 1)
+    iota(V("cmod", 0, NU), [[0, 24], [1, 16]], 0, 0)
+    iota(V("t6", 0, 6), [[16, 6]], NU, 0)
+    iota(V("jown", 0, NT), [[1, NT]], OWN, 0)
+    iota(V("jpar", 0, NT), [[1, NT]], PAR, 0)
+    memset(V("xtile", 0, 4 * XC), 0.0)
+    memset(V("tr1", 0, 512), 1.0)
+    ts(V("pmi", 0, 1), V("ip", 0, 1), 15, A.bitwise_and)
+    ts(V("pdi", 0, 1), V("ip", 0, 1), 4, A.logical_shift_right)
+    copy(V("pm", 0, 1), V("pmi", 0, 1))
+    copy(V("pd", 0, 1), V("pdi", 0, 1))
+    memset(V("mask36", 0, 36), 0.0)
+    memset(V("xt0", 384, 512), 0.0)
+    memset(V("xt1", 384, 512), 0.0)
+    memset(V("negc", 0, 128), -1e29)
+    ts(V("z1", 0, 520), V("iotac", 0, 520), V("p4", 0, 1), A.is_equal)
+    ts(V("mask", 0, NT), V("iotac", 0, NT), V("pcol", 0, 1), A.is_equal)
+    ts(V("mask", NT, XL), V("iotac", 0, 6), V("pd", 0, 1), A.is_equal)
+    ts(V("tr1", 3, 512, 4), V("iotac", 0, 128), V("pcol", 0, 1), A.is_le, 512.0, A.mult)
+    ts(V("eq16", 0, 128), V("cmod", 0, 128), V("pm", 0, 1), A.is_equal)
+    for n, c in (("e25", 0.25), ("e75", 0.75)):
+        copy(V("z" + n, 0, 520), V("z1", 0, 520), "scalar", scale=c)
+    copy(V("xtile", 3, 4 * NT, 4), V("mask", 0, NT), "scalar")
+    copy(V("mb", 0, XL), V("mask", 0, XL), "scalar", scale=1024.0, bias=-1024.0)
+    for t in range(4):
+        copy(V("tr16", t, 512, 4), V("eq16", 0, 128), "scalar", scale=16.0 if t == 3 else 1.0)
+    for t in range(4):
+        copy(V("tnegw", t, 512, 4), V("eq16", 0, 128), "scalar", scale=0.0, bias=0.0 if t == 3 else -1.0)
+    copy(V("mask36", 0, 24, 4), V("mask", NT, XL), "scalar")
+    copy(V("mask36", 24, 36, 4), V("mask", NT, NT + 3), "scalar")
+    copy(V("mask36", 27, 36, 4), V("mask", NT + 3, XL), "scalar")
+    copy(V("ftile", 0, 512), V("iotac", 0, 512), "scalar", scale=0.0)
+    copy(V("mslot0", 0, NU), V("iotac", 0, NU), "scalar", scale=0.0)
+    ts(V("diagm", 0, NU), V("cmod", 0, NU), V("pm", 0, 1), A.is_equal)
+    quant(V("r1", 0, 128), V("tr1", 0, 512))
+    ts(V("t6", 0, 6), V("t6", 0, 6), V("pm", 0, 1), A.add)
+    tt(V("src0", 0, NU), V("iotac", 0, NU), V("diagm", 0, NU), A.mult)
+    quant(V("xq0", 0, 128), V("xt0", 0, 512))
+    lay(V("sel", 96, 128), V("xq0", 96, 128))
+    lay(V("selm", 0, 32), V("xq0", 96, 128))
+
+    def etile(n, t):
+        quant(V(n, 128 * t, 128 * t + 128), V("z" + n, 4 - t, 516 - t))
+
+    for t in range(4):
+        etile("e25", t)
+    BANK = (4, 5, 6)
+
+    def score(b, m):
+        mm(BANK[m], V("xq%d" % b, 0, 128), V("tab%d" % b, 128 * m, 128 * m + 128))
+
+    def run_max(m):
+        scan(V("p", 128 * m, 128 * m + 128), V("ps%d" % BANK[m], 0, 128), V("negc", 0, 128),
+             V("p", 128 * m - 1, 128 * m) if m else -1e29, A.max, A.max)
+
+    def load_units(m):
+        quant(V("tab0", 128 * m, 128 * m + 128), V("kbt", 512 * m, 512 * m + 512))
+        score(0, m)
+
+    load_units(0)
+    etile("e75", 0)
+    etile("e75", 1)
+    load_units(1)
+    quant(V("r16", 0, 128), V("tr16", 0, 512))
+    run_max(0)
+    load_units(2)
+    etile("e75", 2)
+    run_max(1)
+    quant(V("negw", 0, 128), V("tnegw", 0, 512))
+    etile("e75", 3)
+    run_max(2)
+
+    for b in range(NR):
+        tab, xq, nxt = "tab%d" % b, "xq%d" % b, "tab%d" % (b + 1) if b + 1 < NR else "fin"
+        win, mslot, src = "win%d" % b, "mslot%d" % b, "src%d" % b
+        lown, land, lx, lxp = [V("%s%d" % (n, b), 0, 6) for n in ("lown", "land", "lx", "lxp")]
+        partner = T.cores[rank ^ (1 << b)]
+        for t in range(4):
+            mm(t, V("e25", 128 * t, 128 * t + 128), V(xq, 0, 128), True, False)
+        last = V("p", NU - 1, NU)
+        _record(rec, "scalar", "comp",
+                lambda q, w=win: q.activation(T.junk[:, 0:NU], T.p[:, 0:NU], AF.Sign, bias=T.p[:, NU - 1:NU], scale=-1.0,
+                                              accum_out=T[w][:, 0:1]), [V("p", 0, NU)], [V("junk", 0, NU), V(win, 0, 1)])
+        ts(V("zz", 0, 24), V("p", 15, NU, 16), last, A.is_lt, 16.0, A.mult)
+        reduce(V("h1", 0, 1), V("zz", 0, 12), A.add)
+        reduce(V("h2", 0, 1), V("zz", 12, 24), A.add)
+        ts(V("mbh", 0, XL), V("mb", 0, XL), V("h1", 0, 1), A.subtract, V("h2", 0, 1), A.subtract)
+        ts(V("xtile", 1, 4 * XL, 4), V("mask", 0, XL), V("h1", 0, 1), A.mult)
+        ts(V("xtile", 2, 4 * XL, 4), V("mask", 0, XL), V("h2", 0, 1), A.mult)
+        ts(V("xtile", 0, 4 * XL, 4), V("mbh", 0, XL), V(win, 0, 1), A.add, 0.0, A.max)
+        quant(V("xl", 0, XC), V("xtile", 0, 4 * XC))
+        mm(5, V("r16", 0, 128), V("xl", 0, XC))
+        mm(6, V("r1", 0, 128), V("xl", 0, XC), True, False)
+        mm(6, V("xl", 0, XC), V("negw", 0, 128), False, True)
+        copy(lown, V("ps5", NT, XL))
+        send(partner, land, lown, "al%d" % b, "ll")
+        pick(V("sel", 0, NT), V(tab, 0, NU), lown)
+        for t in range(4):
+            mm(t, V("e75", 128 * t, 128 * t + 128), V("sel", 0, 128), False, True)
+        tt(V("d6", 0, 6), V("ps5", NT, XL), V("t6", 0, 6), A.subtract)
+        reduce(V("dmin", 0, 1), V("ps6", 0, NT), A.min, absv=True)
+        ts(V("ftile", 0, 36), V("mask36", 0, 36), V("dmin", 0, 1), A.mult, 1.0, A.min)
+        quant(V("xf", 0, 128), V("ftile", 0, 512))
+        mm(7, V("r16", 0, 128), V("xf", 0, 128))
+        for t in range(3):
+            copy(V("nt", t, 512, 4), V("ps%d" % t, 0, 128), "scalar")
+        if b == 1:
+            copy(V("fsend", 0, 4), V("ps7", 6, 10), "scalar")
+            send(partner, V("fland", 0, 4), V("fsend", 0, 4), "af1", "lf")
+            tt(V("mval", 0, NT), V("diagm", 0, NU), V("jown", 0, NT), A.mult, off=lown)
+        copy(V("nt", 3, 512, 4), V("ps3", 0, 128))
+        quant(V(tab, OWN, OWN + 128), V("nt", 0, 512))
+        for x in (tab, tab + "s"):
+            send(partner, V(x, PAR, PAR + NT), V(x, OWN, OWN + NT), "ac%d" % b, "lc")
+        tt(V("tx", 0, 6), V("ps7", 0, 6), V("d6", 0, 6), A.mult)
+        tt(V("tx2", 0, 6), V("tx", 0, 6), V("t6", 0, 6), A.add)
+        copy(lx, V("tx2", 0, 6))
+        if b == 0:
+            send(partner, lxp, lx, "af0", "lf")
+            copy(V("ze50", 0, 520), V("z1", 0, 520), "scalar", scale=0.5)
+            copy(V("src1", 0, NU), V("src0", 0, NU), "scalar")
+            copy(V("reset", 0, NU), V("cmod", 0, NU), "scalar", func=AF.Sign)
+        store("sync", T.ch[b:b + 1, 0:NT], V(win, 0, 1), T[win][0:NT, 0:1])
+        scatter(V(mslot, 0, 480), lx, V("jown", 0, NT))
+        copy(V("mf1", 0, NU), V(mslot, 0, NU), "scalar", func=AF.Sign)
+        copy(V("mflag", 0, NU), V("mf1", 0, NU), "scalar", scale=float(MRG - PAR))
+        if b == 0:
+            tt(V("mval", 0, NT), V("diagm", 0, NU), V("jown", 0, NT), A.mult, off=lown)
+            copy(V("mslot1", 0, NU), V("iotac", 0, NU), "scalar", scale=0.0)
+            copy(V("t6s", 0, 3), V("t6", 0, 3), "scalar")
+            copy(V("t6s", 3, 6), V("t6", 3, 6), "scalar", scale=-0.0625)
+            scatter(V(src, 0, 480), lx, V("mval", 0, NT))
+            for t in range(4):
+                etile("e50", t)
+            quant(V("xq1", 0, 128), V("xt1", 0, 512))
+            quant(V("wq", 0, 128), V("wt", 0, 512))
+        arrive([land], "al%d" % b, partner)
+        tt(V("c1", 0, NT), V(mslot, 0, NU), V("diagm", 0, NT), A.mult, off=land)
+        if b == 1:
+            scatter(V(src, 0, 480), lx, V("mval", 0, NT))
+        scan(V("c2", 0, NT), V("reset", 0, NT), V("c1", 0, NT), 0.0, A.mult, A.add)
+        if b == 1:
+            copy(V("lpf", 0, 3), V(land[0], 0, 3))
+        copy(V("clist", 0, 6), V("c2", 15, NT, 16))
+        if b == 1:
+            ts(V("lpf", 3, 6), V(land[0], 3, 6), -0.0625, A.mult)
+        pick(V("selm", 32, 128), V(tab, 0, PAR), V("clist", 0, 6))
+        for t in range(4):
+            mm(t, V("e50", 128 * t, 128 * t + 128), V("selm", 0, 128), True, False)
+        arrive([V(tab, PAR, PAR + NT), V(tab + "s", PAR, PAR + NT)], "ac%d" % b, partner, 2)
+        for t in range(4):
+            mm(t, V("e50", 128 * t, 128 * t + 128), V(tab, PAR - 32, PAR + NT), False, True)
+        tt(V("val", 0, NT), V("mflag", 0, NU), V("jpar", 0, NT), A.add, off=land)
+        if b == 1:
+            tt(V("d6p", 0, 6), V("lpf", 0, 6), V("t6s", 0, 6), A.subtract)
+            arrive([V("fland", 0, 4)], "af1", partner)
+            ts(V("fb", 3, 6), V("fland", 0, 3), 8.0, A.is_ge, -16.0, A.mult)
+            tt(V("pval", 0, NT), V("diagm", 0, NU), V("val", 0, NT), A.mult, off=land)
+            tt(V("fb", 0, 3), V("fland", 0, 3), V("fb", 3, 6), A.add)
+            tt(V("txp", 0, 6), V("fb", 0, 6), V("d6p", 0, 6), A.mult)
+            tt(V("txp2", 0, 6), V("txp", 0, 6), V("t6", 0, 6), A.add)
+            copy(lxp, V("txp2", 0, 6))
+        else:
+            tt(V("pval", 0, NT), V("diagm", 0, NU), V("val", 0, NT), A.mult, off=land)
+            arrive([lxp], "af0", partner)
+        scatter(V(src, 0, 480), lxp, V("pval", 0, NT))
+        scan(V("srcs", 0, NU), V("reset", 0, NU), V(src, 0, NU), 0.0, A.mult, A.add)
+        copy(V("blist", 0, 24), V("srcs", 15, NU, 16))
+        for t in range(4):
+            copy(V("mt", t, 512, 4), V("ps%d" % t, 0, 128), "scalar")
+        quant(V(tab, MQ, MQ + 128), V("mt", 0, 512))
+        for m in range(3):
+            pick(V(nxt, 128 * m, 128 * m + 128), V(tab, 0, WIN), V("blist", 8 * m, 8 * m + 8))
+            if b + 1 < NR:
+                score(b + 1, m)
+        if b + 1 < NR:
+            for m in range(3):
+                run_max(m)
+
+    for m in range(3):
+        mm(BANK[m], V("wq", 0, 128), V("fin", 128 * m, 128 * m + 128))
+    for a, b in ((0, 256), (256, NU)):
+        store("sync", T.oc[:, 4 * a:4 * b], V("fin", a, b), T.fin[:, a:b].bitcast(dt.uint8))
+    for m in range(3):
+        copy(V("ysb", 128 * m, 128 * m + 128), V("ps%d" % BANK[m], 0, 128), "scalar" if m == 1 else "vector")
+    for a, b in ((0, 256), (256, NU)):
+        store("sync", T.y[:, a:b], V("ysb", a, b), T.ysb[:, a:b])
+    for k in range(4):
+        store("scalar", T.osc[4 * k:4 * k + 4, 0:NU], V("fins", 0, NU), T.fins[32 * k:32 * k + 4, 0:NU])
+    _record(rec, "sync", "end", None, [], [], extra=stores)
+    _issue(rec, {"vector": g.vector, "scalar": g.scalar, "tensor": g.tensor, "gpsimd": g, "sync": g.sync}, T.sem)
+    n = sum(len(topo.engines(core, T.cores[rank ^ (1 << b)])) for b in range(NR))
+    g.wait_ge(T.sem.ll, n)
+    g.wait_ge(T.sem.lc, 2 * n)
+    g.wait_ge(T.sem.lf, n)

@@ -6,6 +6,7 @@ NU, NT, NR = 384, 96, 2
 OWN, PAR, MRG, WIN = 384, 512, 640, 736
 MQ = 608
 XC, XL = 128, 102
+PIECES = ((4, 0, 128), (5, 128, 256), (6, 256, NU))
 F4, F32, BF, U16, I32, U8 = "float8_e4m3fn_x4", "float32", "bfloat16", "uint16", "int32", "uint8"
 
 
@@ -38,15 +39,15 @@ def _decl():
     pair("fin", NU)
     for n in range(8):
         add("ps%d" % n, 512, F32, "psum")
-    for n, w, t in (("kbt", 1536, BF), ("wt", 512, BF), ("nt", 512, BF), ("mt", 512, BF), ("xtile", 4 * XC, BF), ("ftile", 512, BF),
+    for n, w, t in (("kbt", 1536, BF), ("wt", 512, BF), ("nt", 512, BF), ("mt", 512, BF), ("xtile", 4 * XC, BF), ("ones", 520, BF),
                     ("fsend", 4, BF), ("fland", 4, BF), ("z1", 520, BF), ("mask", XL, BF), ("mask36", 36, BF), ("eq16", 128, BF),
-                    ("junk", NU, BF), ("mb", XL, BF), ("mbh", XL, BF), ("ip", 1, I32), ("pmi", 1, I32), ("pdi", 1, I32),
+                    ("junk", NU, BF), ("mb", XL, BF), ("mbh", XL, BF), ("mb2", XL, BF), ("ip", 1, I32), ("pmi", 1, I32), ("pdi", 1, I32),
                     ("clist", 6, U16), ("blist", 24, U16)):
         add(n, w, t)
-    for n, w in (("iotac", 520), ("cmod", NU), ("jown", NT), ("jpar", NT), ("t6", 6), ("t6s", 6), ("pcol", 1), ("p4", 1), ("pm", 1),
-                 ("pd", 1), ("negc", 128), ("diagm", NU), ("reset", NU), ("p", NU), ("zz", 24), ("h1", 1), ("h2", 1), ("dmin", 1),
-                 ("d6", 6), ("tx", 6), ("tx2", 6), ("mval", NT), ("mf1", NU), ("mflag", NU), ("c1", NT), ("c2", NT), ("val", NT),
-                 ("pval", NT), ("lpf", 6), ("d6p", 6), ("fb", 6), ("txp", 6), ("txp2", 6), ("srcs", NU), ("ysb", NU)):
+    for n, w in (("iotac", NU), ("cmod", NU), ("jown", NT), ("jpar", NT), ("t6", 6), ("t6s", 6), ("pcol", 1), ("pm", 1),
+                 ("pd", 1), ("negc", 128), ("diagm", NU), ("reset", NU), ("p", NU), ("zz", 24), ("h1", 1), ("dmin", 1),
+                 ("d6", 6), ("mval", NT), ("mf1", NU), ("mflag", NU), ("c1", NT), ("c2", NT), ("val", NT),
+                 ("pval", NT), ("lpf", 6), ("d6p", 6), ("fb", 6), ("srcs", NU), ("ysb", NU)):
         add(n, w, F32)
     return s
 
@@ -147,6 +148,9 @@ def rank_program(g, core, T, topo):
     def val(x):
         return ap(x) if isinstance(x, tuple) else x
 
+    def lanes(src, dst):
+        return topo.engines(src, dst)[::2]
+
     def memset(out, c):
         _record(rec, "vector", "comp", lambda q: q.memset(ap(out), c), [], [out])
 
@@ -213,8 +217,8 @@ def rank_program(g, core, T, topo):
             return q.iota(ap(out), pattern, base, cm)
         _record(rec, "gpsimd", "comp", call, [], [out])
 
-    def load(queue, out, src):
-        _record(rec, queue, "dma", lambda q: q.dma_start(ap(out), src), [], [out])
+    def load(queue, out, src, after=()):
+        return _record(rec, queue, "dma", lambda q: q.dma_start(ap(out), src), [], [out], after)
 
     def lay(out, in_):
         _record(rec, "sync", "dma", lambda q: q.dma_start(ap(out).bitcast(dt.uint8), ap(in_).bitcast(dt.uint8)), [in_], [out])
@@ -233,23 +237,23 @@ def rank_program(g, core, T, topo):
             o, i = ap(out), ap(in_)
             if codes:
                 o, i = o.bitcast(dt.uint8), i.bitcast(dt.uint8)
-            return q.remote_dma(o, i, T.sem[arr], T.sem[loc], pid, rid, topo.mask(core, dst))
+            return q.remote_dma(o, i, T.sem[arr], T.sem[loc], pid, rid, sum(1 << e for e in lanes(core, dst)))
         _record(rec, "gpsimd", "remote", call, [in_], [])
 
     def arrive(writes, sem, src, calls=1):
-        _record(rec, "network", "arr", (sem, calls * len(topo.engines(src, core))), [], writes)
+        _record(rec, "network", "arr", (sem, calls * len(lanes(src, core))), [], writes)
 
     load("sync", V("xt0", 0, 384), T.x[:, 0:384])
     load("scalar", V("kbt", 0, 512), T.kb[:, 0:512])
     load("sync", V("kbt", 512, 1024), T.kb[:, 512:1024])
-    load("scalar", V("kbt", 1024, 1536), T.kb[:, 1024:1536])
-    load("sync", V("xt1", 0, 384), T.x[:, 384:768])
-    load("sync", V("wt", 0, 512), T.w[:, 0:512])
+    kb2 = load("scalar", V("kbt", 1024, 1536), T.kb[:, 1024:1536])
 
-    iota(V("p4", 0, 1), [[0, 1]], 4, 4)
+    memset(V("ones", 0, 520), 1.0)
     iota(V("ip", 0, 1), [[0, 1]], 0, 1)
-    iota(V("iotac", 0, 520), [[1, 520]], 0, 0)
     iota(V("pcol", 0, 1), [[0, 1]], 0, 1)
+    _record(rec, "gpsimd", "comp", lambda q: q.affine_select(T.z1[:, 0:520], T.ones[:, 0:520], [[-1, 520]], A.is_equal, 0.0, 4, 4),
+            [V("ones", 0, 520)], [V("z1", 0, 520)])
+    iota(V("iotac", 0, NU), [[1, NU]], 0, 0)
     iota(V("cmod", 0, NU), [[0, 24], [1, 16]], 0, 0)
     iota(V("t6", 0, 6), [[16, 6]], NU, 0)
     iota(V("jown", 0, NT), [[1, NT]], OWN, 0)
@@ -262,64 +266,60 @@ def rank_program(g, core, T, topo):
     copy(V("pd", 0, 1), V("pdi", 0, 1))
     memset(V("mask36", 0, 36), 0.0)
     memset(V("xt0", 384, 512), 0.0)
-    memset(V("xt1", 384, 512), 0.0)
     memset(V("negc", 0, 128), -1e29)
-    ts(V("z1", 0, 520), V("iotac", 0, 520), V("p4", 0, 1), A.is_equal)
-    ts(V("mask", 0, NT), V("iotac", 0, NT), V("pcol", 0, 1), A.is_equal)
-    ts(V("mask", NT, XL), V("iotac", 0, 6), V("pd", 0, 1), A.is_equal)
-    ts(V("tr1", 3, 512, 4), V("iotac", 0, 128), V("pcol", 0, 1), A.is_le, 512.0, A.mult)
-    ts(V("eq16", 0, 128), V("cmod", 0, 128), V("pm", 0, 1), A.is_equal)
+    memset(V("xt1", 384, 512), 0.0)
     for n, c in (("e25", 0.25), ("e75", 0.75)):
         copy(V("z" + n, 0, 520), V("z1", 0, 520), "scalar", scale=c)
-    copy(V("xtile", 3, 4 * NT, 4), V("mask", 0, NT), "scalar")
-    copy(V("mb", 0, XL), V("mask", 0, XL), "scalar", scale=1024.0, bias=-1024.0)
-    for t in range(4):
-        copy(V("tr16", t, 512, 4), V("eq16", 0, 128), "scalar", scale=16.0 if t == 3 else 1.0)
-    for t in range(4):
-        copy(V("tnegw", t, 512, 4), V("eq16", 0, 128), "scalar", scale=0.0, bias=0.0 if t == 3 else -1.0)
-    copy(V("mask36", 0, 24, 4), V("mask", NT, XL), "scalar")
-    copy(V("mask36", 24, 36, 4), V("mask", NT, NT + 3), "scalar")
-    copy(V("mask36", 27, 36, 4), V("mask", NT + 3, XL), "scalar")
-    copy(V("ftile", 0, 512), V("iotac", 0, 512), "scalar", scale=0.0)
-    copy(V("mslot0", 0, NU), V("iotac", 0, NU), "scalar", scale=0.0)
-    ts(V("diagm", 0, NU), V("cmod", 0, NU), V("pm", 0, 1), A.is_equal)
-    quant(V("r1", 0, 128), V("tr1", 0, 512))
-    ts(V("t6", 0, 6), V("t6", 0, 6), V("pm", 0, 1), A.add)
-    tt(V("src0", 0, NU), V("iotac", 0, NU), V("diagm", 0, NU), A.mult)
-    quant(V("xq0", 0, 128), V("xt0", 0, 512))
-    lay(V("sel", 96, 128), V("xq0", 96, 128))
-    lay(V("selm", 0, 32), V("xq0", 96, 128))
 
     def etile(n, t):
         quant(V(n, 128 * t, 128 * t + 128), V("z" + n, 4 - t, 516 - t))
 
     for t in range(4):
         etile("e25", t)
-    BANK = (4, 5, 6)
+    ts(V("mask", 0, NT), V("iotac", 0, NT), V("pcol", 0, 1), A.is_equal)
+    ts(V("mask", NT, XL), V("iotac", 0, 6), V("pd", 0, 1), A.is_equal)
+    ts(V("tr1", 3, 512, 4), V("iotac", 0, 128), V("pcol", 0, 1), A.is_le, 512.0, A.mult)
+    copy(V("xtile", 3, 4 * NT, 4), V("mask", 0, NT), "scalar")
+    copy(V("mb", 0, XL), V("mask", 0, XL), "scalar", scale=1024.0, bias=-1024.0)
+    copy(V("mb2", 0, XL), V("mask", 0, XL), "scalar", scale=1024.0, bias=-1024.0 - 192.0)
+    copy(V("mask36", 0, 24, 4), V("mask", NT, XL), "scalar")
+    copy(V("mask36", 24, 36, 4), V("mask", NT, NT + 3), "scalar")
+    copy(V("mask36", 27, 36, 4), V("mask", NT + 3, XL), "scalar")
+    ts(V("eq16", 0, 128), V("cmod", 0, 128), V("pm", 0, 1), A.is_equal)
+    for t in range(4):
+        copy(V("tr16", t, 512, 4), V("eq16", 0, 128), "scalar", scale=16.0 if t == 3 else 1.0)
+    for t in range(4):
+        copy(V("tnegw", t, 512, 4), V("eq16", 0, 128), "scalar", scale=0.0, bias=0.0 if t == 3 else -1.0)
+    copy(V("mslot0", 0, NU), V("iotac", 0, NU), "scalar", scale=0.0)
+    quant(V("r1", 0, 128), V("tr1", 0, 512))
+    ts(V("t6", 0, 6), V("t6", 0, 6), V("pm", 0, 1), A.add)
+    ts(V("diagm", 0, NU), V("cmod", 0, NU), V("pm", 0, 1), A.is_equal)
+    quant(V("xq0", 0, 128), V("xt0", 0, 512))
+    lay(V("sel", 96, 128), V("xq0", 96, 128))
+    lay(V("selm", 0, 32), V("xq0", 96, 128))
+    load("sync", V("xt1", 0, 384), T.x[:, 384:768], [kb2])
+    load("sync", V("wt", 0, 512), T.w[:, 0:512], [kb2])
 
-    def score(b, m):
-        mm(BANK[m], V("xq%d" % b, 0, 128), V("tab%d" % b, 128 * m, 128 * m + 128))
+    def score(b, ps, u, v):
+        mm(ps, V("xq%d" % b, 0, 128), V("tab%d" % b, u, v))
 
-    def run_max(m):
-        scan(V("p", 128 * m, 128 * m + 128), V("ps%d" % BANK[m], 0, 128), V("negc", 0, 128),
-             V("p", 128 * m - 1, 128 * m) if m else -1e29, A.max, A.max)
+    def run_max(ps, u, v):
+        scan(V("p", u, v), V("ps%d" % ps, 0, v - u), V("negc", 0, v - u), V("p", u - 1, u) if u else -1e29, A.max, A.max)
 
-    def load_units(m):
-        quant(V("tab0", 128 * m, 128 * m + 128), V("kbt", 512 * m, 512 * m + 512))
-        score(0, m)
+    def units(ps, u, v):
+        quant(V("tab0", u, v), V("kbt", 4 * u, 4 * v))
+        score(0, ps, u, v)
 
-    load_units(0)
-    etile("e75", 0)
-    etile("e75", 1)
-    load_units(1)
+    units(*PIECES[0])
     quant(V("r16", 0, 128), V("tr16", 0, 512))
-    run_max(0)
-    load_units(2)
-    etile("e75", 2)
-    run_max(1)
+    run_max(*PIECES[0])
+    etile("e75", 0)
+    units(*PIECES[1])
+    etile("e75", 1)
+    run_max(*PIECES[1])
+    units(*PIECES[2])
     quant(V("negw", 0, 128), V("tnegw", 0, 512))
-    etile("e75", 3)
-    run_max(2)
+    run_max(*PIECES[2])
 
     for b in range(NR):
         tab, xq, nxt = "tab%d" % b, "xq%d" % b, "tab%d" % (b + 1) if b + 1 < NR else "fin"
@@ -333,13 +333,18 @@ def rank_program(g, core, T, topo):
                 lambda q, w=win: q.activation(T.junk[:, 0:NU], T.p[:, 0:NU], AF.Sign, bias=T.p[:, NU - 1:NU], scale=-1.0,
                                               accum_out=T[w][:, 0:1]), [V("p", 0, NU)], [V("junk", 0, NU), V(win, 0, 1)])
         ts(V("zz", 0, 24), V("p", 15, NU, 16), last, A.is_lt, 16.0, A.mult)
-        reduce(V("h1", 0, 1), V("zz", 0, 12), A.add)
-        reduce(V("h2", 0, 1), V("zz", 12, 24), A.add)
-        ts(V("mbh", 0, XL), V("mb", 0, XL), V("h1", 0, 1), A.subtract, V("h2", 0, 1), A.subtract)
-        ts(V("xtile", 1, 4 * XL, 4), V("mask", 0, XL), V("h1", 0, 1), A.mult)
-        ts(V("xtile", 2, 4 * XL, 4), V("mask", 0, XL), V("h2", 0, 1), A.mult)
+        reduce(V("h1", 0, 1), V("zz", 0, 24), A.add)
+        ts(V("mbh", 0, XL), V("mb", 0, XL), V("h1", 0, 1), A.subtract)
+        ts(V("xtile", 1, 4 * XL, 4), V("mask", 0, XL), V("h1", 0, 1), A.mult, 192.0, A.min)
+        _record(rec, "scalar", "comp", lambda q: q.activation(T.xtile[:, 2:4 * XL:4], T.mb2[:, 0:XL], AF.Relu, bias=T.h1[:, 0:1]),
+                [V("mb2", 0, XL), V("h1", 0, 1)], [V("xtile", 2, 4 * XL, 4)])
         ts(V("xtile", 0, 4 * XL, 4), V("mbh", 0, XL), V(win, 0, 1), A.add, 0.0, A.max)
         quant(V("xl", 0, XC), V("xtile", 0, 4 * XC))
+        if b == 0:
+            etile("e75", 2)
+            etile("e75", 3)
+        else:
+            quant(V("wq", 0, 128), V("wt", 0, 512))
         mm(5, V("r16", 0, 128), V("xl", 0, XC))
         mm(6, V("r1", 0, 128), V("xl", 0, XC), True, False)
         mm(6, V("xl", 0, XC), V("negw", 0, 128), False, True)
@@ -348,28 +353,26 @@ def rank_program(g, core, T, topo):
         pick(V("sel", 0, NT), V(tab, 0, NU), lown)
         for t in range(4):
             mm(t, V("e75", 128 * t, 128 * t + 128), V("sel", 0, 128), False, True)
-        tt(V("d6", 0, 6), V("ps5", NT, XL), V("t6", 0, 6), A.subtract)
         reduce(V("dmin", 0, 1), V("ps6", 0, NT), A.min, absv=True)
-        ts(V("ftile", 0, 36), V("mask36", 0, 36), V("dmin", 0, 1), A.mult, 1.0, A.min)
-        quant(V("xf", 0, 128), V("ftile", 0, 512))
+        tt(V("d6", 0, 6), V("ps5", NT, XL), V("t6", 0, 6), A.subtract)
+        ts(V("xtile", 4 * XL, 4 * XL + 36), V("mask36", 0, 36), V("dmin", 0, 1), A.mult, 1.0, A.min)
+        quant(V("xf", 0, 128), V("xtile", 0, 512))
         mm(7, V("r16", 0, 128), V("xf", 0, 128))
         for t in range(3):
             copy(V("nt", t, 512, 4), V("ps%d" % t, 0, 128), "scalar")
         if b == 1:
-            copy(V("fsend", 0, 4), V("ps7", 6, 10), "scalar")
+            copy(V("fsend", 0, 4), V("ps7", XL + 6, XL + 10), "scalar")
             send(partner, V("fland", 0, 4), V("fsend", 0, 4), "af1", "lf")
             tt(V("mval", 0, NT), V("diagm", 0, NU), V("jown", 0, NT), A.mult, off=lown)
         copy(V("nt", 3, 512, 4), V("ps3", 0, 128))
         quant(V(tab, OWN, OWN + 128), V("nt", 0, 512))
         for x in (tab, tab + "s"):
             send(partner, V(x, PAR, PAR + NT), V(x, OWN, OWN + NT), "ac%d" % b, "lc")
-        tt(V("tx", 0, 6), V("ps7", 0, 6), V("d6", 0, 6), A.mult)
-        tt(V("tx2", 0, 6), V("tx", 0, 6), V("t6", 0, 6), A.add)
-        copy(lx, V("tx2", 0, 6))
+        for k in range(6):
+            ts(V(lx[0], k, k + 1), V("d6", k, k + 1), V("ps7", XL + k, XL + k + 1), A.mult, V("t6", k, k + 1), A.add)
         if b == 0:
             send(partner, lxp, lx, "af0", "lf")
             copy(V("ze50", 0, 520), V("z1", 0, 520), "scalar", scale=0.5)
-            copy(V("src1", 0, NU), V("src0", 0, NU), "scalar")
             copy(V("reset", 0, NU), V("cmod", 0, NU), "scalar", func=AF.Sign)
         store("sync", T.ch[b:b + 1, 0:NT], V(win, 0, 1), T[win][0:NT, 0:1])
         scatter(V(mslot, 0, 480), lx, V("jown", 0, NT))
@@ -380,67 +383,70 @@ def rank_program(g, core, T, topo):
             copy(V("mslot1", 0, NU), V("iotac", 0, NU), "scalar", scale=0.0)
             copy(V("t6s", 0, 3), V("t6", 0, 3), "scalar")
             copy(V("t6s", 3, 6), V("t6", 3, 6), "scalar", scale=-0.0625)
-            scatter(V(src, 0, 480), lx, V("mval", 0, NT))
             for t in range(4):
                 etile("e50", t)
-            quant(V("xq1", 0, 128), V("xt1", 0, 512))
-            quant(V("wq", 0, 128), V("wt", 0, 512))
+            tt(V("src0", 0, NU), V("iotac", 0, NU), V("diagm", 0, NU), A.mult)
+            copy(V("src1", 0, NU), V("src0", 0, NU), "scalar")
         arrive([land], "al%d" % b, partner)
-        tt(V("c1", 0, NT), V(mslot, 0, NU), V("diagm", 0, NT), A.mult, off=land)
-        if b == 1:
+        arrive([V(tab, PAR, PAR + NT), V(tab + "s", PAR, PAR + NT)], "ac%d" % b, partner, 2)
+        arrive([lxp] if b == 0 else [V("fland", 0, 4)], "af%d" % b, partner)
+        value = (V("val", 0, NT), V("mflag", 0, NU), V("jpar", 0, NT), A.add, land)
+        masked = (V("pval", 0, NT), V("diagm", 0, NU), V("val", 0, NT), A.mult, land)
+        tt(V("c1", 0, NT), V(mslot, 0, NU), V("diagm", 0, NT), A.mult, land)
+        if b == 0:
+            tt(*value)
+        else:
             scatter(V(src, 0, 480), lx, V("mval", 0, NT))
         scan(V("c2", 0, NT), V("reset", 0, NT), V("c1", 0, NT), 0.0, A.mult, A.add)
-        if b == 1:
+        if b == 0:
+            tt(*masked)
+        else:
             copy(V("lpf", 0, 3), V(land[0], 0, 3))
+            ts(V("lpf", 3, 6), V(land[0], 3, 6), -0.0625, A.mult)
         copy(V("clist", 0, 6), V("c2", 15, NT, 16))
         if b == 1:
-            ts(V("lpf", 3, 6), V(land[0], 3, 6), -0.0625, A.mult)
-        pick(V("selm", 32, 128), V(tab, 0, PAR), V("clist", 0, 6))
-        for t in range(4):
-            mm(t, V("e50", 128 * t, 128 * t + 128), V("selm", 0, 128), True, False)
-        arrive([V(tab, PAR, PAR + NT), V(tab + "s", PAR, PAR + NT)], "ac%d" % b, partner, 2)
-        for t in range(4):
-            mm(t, V("e50", 128 * t, 128 * t + 128), V(tab, PAR - 32, PAR + NT), False, True)
-        tt(V("val", 0, NT), V("mflag", 0, NU), V("jpar", 0, NT), A.add, off=land)
-        if b == 1:
             tt(V("d6p", 0, 6), V("lpf", 0, 6), V("t6s", 0, 6), A.subtract)
-            arrive([V("fland", 0, 4)], "af1", partner)
-            ts(V("fb", 3, 6), V("fland", 0, 3), 8.0, A.is_ge, -16.0, A.mult)
-            tt(V("pval", 0, NT), V("diagm", 0, NU), V("val", 0, NT), A.mult, off=land)
-            tt(V("fb", 0, 3), V("fland", 0, 3), V("fb", 3, 6), A.add)
-            tt(V("txp", 0, 6), V("fb", 0, 6), V("d6p", 0, 6), A.mult)
-            tt(V("txp2", 0, 6), V("txp", 0, 6), V("t6", 0, 6), A.add)
-            copy(lxp, V("txp2", 0, 6))
+        pick(V("selm", 32, 128), V(tab, 0, PAR), V("clist", 0, 6))
+        own, par = V("selm", 0, 128), V(tab, PAR - 32, PAR + NT)
+        for k, x in enumerate((par, own) if b == 0 else (own, par)):
+            for t in range(4):
+                mm(t, V("e50", 128 * t, 128 * t + 128), x, k == 0, k == 1)
+        if b == 0:
+            scatter(V(src, 0, 480), lx, V("mval", 0, NT))
         else:
-            tt(V("pval", 0, NT), V("diagm", 0, NU), V("val", 0, NT), A.mult, off=land)
-            arrive([lxp], "af0", partner)
+            tt(*value)
+            ts(V("fb", 3, 6), V("fland", 0, 3), 8.0, A.is_ge, -16.0, A.mult)
+            tt(*masked)
+            tt(V("fb", 0, 3), V("fland", 0, 3), V("fb", 3, 6), A.add)
+            for k in (3, 4, 5, 0, 1, 2):
+                ts(V(lxp[0], k, k + 1), V("d6p", k, k + 1), V("fb", k, k + 1), A.mult, V("t6", k, k + 1), A.add)
         scatter(V(src, 0, 480), lxp, V("pval", 0, NT))
         scan(V("srcs", 0, NU), V("reset", 0, NU), V(src, 0, NU), 0.0, A.mult, A.add)
         copy(V("blist", 0, 24), V("srcs", 15, NU, 16))
+        if b == 0:
+            quant(V("xq1", 0, 128), V("xt1", 0, 512))
         for t in range(4):
             copy(V("mt", t, 512, 4), V("ps%d" % t, 0, 128), "scalar")
         quant(V(tab, MQ, MQ + 128), V("mt", 0, 512))
-        for m in range(3):
-            pick(V(nxt, 128 * m, 128 * m + 128), V(tab, 0, WIN), V("blist", 8 * m, 8 * m + 8))
+        for ps, u, v in PIECES:
+            pick(V(nxt, u, v), V(tab, 0, WIN), V("blist", u // 16, v // 16))
             if b + 1 < NR:
-                score(b + 1, m)
+                score(b + 1, ps, u, v)
         if b + 1 < NR:
-            for m in range(3):
-                run_max(m)
+            for piece in PIECES:
+                run_max(*piece)
 
-    for m in range(3):
-        mm(BANK[m], V("wq", 0, 128), V("fin", 128 * m, 128 * m + 128))
-    for a, b in ((0, 256), (256, NU)):
-        store("sync", T.oc[:, 4 * a:4 * b], V("fin", a, b), T.fin[:, a:b].bitcast(dt.uint8))
-    for m in range(3):
-        copy(V("ysb", 128 * m, 128 * m + 128), V("ps%d" % BANK[m], 0, 128), "scalar" if m == 1 else "vector")
-    for a, b in ((0, 256), (256, NU)):
-        store("sync", T.y[:, a:b], V("ysb", a, b), T.ysb[:, a:b])
+    for ps, u, v in PIECES:
+        mm(ps, V("wq", 0, 128), V("fin", u, v))
+        store("sync", T.oc[:, 4 * u:4 * v], V("fin", u, v), T.fin[:, u:v].bitcast(dt.uint8))
+    for ps, u, v in PIECES:
+        copy(V("ysb", u, v), V("ps%d" % ps, 0, v - u), "scalar" if u == 128 else "vector")
+        store("sync", T.y[:, u:v], V("ysb", u, v), T.ysb[:, u:v])
     for k in range(4):
         store("scalar", T.osc[4 * k:4 * k + 4, 0:NU], V("fins", 0, NU), T.fins[32 * k:32 * k + 4, 0:NU])
-    _record(rec, "sync", "end", None, [], [], extra=stores)
+    _record(rec, "sync", "end", None, [], [], stores)
     _issue(rec, {"vector": g.vector, "scalar": g.scalar, "tensor": g.tensor, "gpsimd": g, "sync": g.sync}, T.sem)
-    n = sum(len(topo.engines(core, T.cores[rank ^ (1 << b)])) for b in range(NR))
+    n = sum(len(lanes(core, T.cores[rank ^ (1 << b)])) for b in range(NR))
     g.wait_ge(T.sem.ll, n)
     g.wait_ge(T.sem.lc, 2 * n)
     g.wait_ge(T.sem.lf, n)

@@ -246,54 +246,56 @@ def rank_program(g, core, T, topo):
     load("sync", V("xt0", 0, 384), T.x[:, 0:384])
     load("scalar", V("kbt", 0, 512), T.kb[:, 0:512])
     load("sync", V("kbt", 512, 1024), T.kb[:, 512:1024])
-    kb2 = load("scalar", V("kbt", 1024, 1536), T.kb[:, 1024:1536])
+    kb2 = load("sync", V("kbt", 1024, 1536), T.kb[:, 1024:1536])
 
-    memset(V("ones", 0, 520), 1.0)
     iota(V("ip", 0, 1), [[0, 1]], 0, 1)
+    iota(V("cmod", 0, NU), [[0, 24], [1, 16]], 0, 0)
     iota(V("pcol", 0, 1), [[0, 1]], 0, 1)
+    iota(V("iotac", 0, NU), [[1, NU]], 0, 0)
+    memset(V("ones", 0, 520), 1.0)
     _record(rec, "gpsimd", "comp", lambda q: q.affine_select(T.z1[:, 0:520], T.ones[:, 0:520], [[-1, 520]], A.is_equal, 0.0, 4, 4),
             [V("ones", 0, 520)], [V("z1", 0, 520)])
-    iota(V("iotac", 0, NU), [[1, NU]], 0, 0)
-    iota(V("cmod", 0, NU), [[0, 24], [1, 16]], 0, 0)
     iota(V("t6", 0, 6), [[16, 6]], NU, 0)
     iota(V("jown", 0, NT), [[1, NT]], OWN, 0)
     iota(V("jpar", 0, NT), [[1, NT]], PAR, 0)
-    memset(V("xtile", 0, 4 * XC), 0.0)
-    memset(V("tr1", 0, 512), 1.0)
     ts(V("pmi", 0, 1), V("ip", 0, 1), 15, A.bitwise_and)
     ts(V("pdi", 0, 1), V("ip", 0, 1), 4, A.logical_shift_right)
     copy(V("pm", 0, 1), V("pmi", 0, 1))
     copy(V("pd", 0, 1), V("pdi", 0, 1))
+    memset(V("xtile", 0, 4 * XC), 0.0)
     memset(V("mask36", 0, 36), 0.0)
-    memset(V("xt0", 384, 512), 0.0)
-    memset(V("negc", 0, 128), -1e29)
-    memset(V("xt1", 384, 512), 0.0)
-    for n, c in (("e25", 0.25), ("e75", 0.75)):
-        copy(V("z" + n, 0, 520), V("z1", 0, 520), "scalar", scale=c)
-
-    def etile(n, t):
-        quant(V(n, 128 * t, 128 * t + 128), V("z" + n, 4 - t, 516 - t))
-
-    for t in range(4):
-        etile("e25", t)
+    ts(V("eq16", 0, 128), V("cmod", 0, 128), V("pm", 0, 1), A.is_equal)
+    ts(V("diagm", 0, NU), V("cmod", 0, NU), V("pm", 0, 1), A.is_equal)
+    memset(V("tr1", 0, 512), 1.0)
     ts(V("mask", 0, NT), V("iotac", 0, NT), V("pcol", 0, 1), A.is_equal)
     ts(V("mask", NT, XL), V("iotac", 0, 6), V("pd", 0, 1), A.is_equal)
     ts(V("tr1", 3, 512, 4), V("iotac", 0, 128), V("pcol", 0, 1), A.is_le, 512.0, A.mult)
+    memset(V("xt0", 384, 512), 0.0)
+    memset(V("negc", 0, 128), -1e29)
+    tt(V("src0", 0, NU), V("iotac", 0, NU), V("diagm", 0, NU), A.mult)
+    quant(V("r1", 0, 128), V("tr1", 0, 512))
+    for t in range(4):
+        copy(V("tr16", t, 512, 4), V("eq16", 0, 128), "scalar", scale=16.0 if t == 3 else 1.0)
     copy(V("xtile", 3, 4 * NT, 4), V("mask", 0, NT), "scalar")
+    for n, c in (("e25", 0.25), ("e75", 0.75)):
+        copy(V("z" + n, 0, 520), V("z1", 0, 520), "scalar", scale=c)
+    for t in range(4):
+        copy(V("tnegw", t, 512, 4), V("eq16", 0, 128), "scalar", scale=0.0, bias=0.0 if t == 3 else -1.0)
     copy(V("mb", 0, XL), V("mask", 0, XL), "scalar", scale=1024.0, bias=-1024.0)
     copy(V("mb2", 0, XL), V("mask", 0, XL), "scalar", scale=1024.0, bias=-1024.0 - 192.0)
     copy(V("mask36", 0, 24, 4), V("mask", NT, XL), "scalar")
     copy(V("mask36", 24, 36, 4), V("mask", NT, NT + 3), "scalar")
     copy(V("mask36", 27, 36, 4), V("mask", NT + 3, XL), "scalar")
-    ts(V("eq16", 0, 128), V("cmod", 0, 128), V("pm", 0, 1), A.is_equal)
-    for t in range(4):
-        copy(V("tr16", t, 512, 4), V("eq16", 0, 128), "scalar", scale=16.0 if t == 3 else 1.0)
-    for t in range(4):
-        copy(V("tnegw", t, 512, 4), V("eq16", 0, 128), "scalar", scale=0.0, bias=0.0 if t == 3 else -1.0)
+    for n, c in (("nt", 4 * NT), ("mt", 0)):
+        copy(V(n, c, c + 128), V("eq16", 0, 128), "scalar", scale=0.0)
     copy(V("mslot0", 0, NU), V("iotac", 0, NU), "scalar", scale=0.0)
-    quant(V("r1", 0, 128), V("tr1", 0, 512))
+
+    def etile(n, t):
+        quant(V(n, 128 * t, 128 * t + 128), V("z" + n, 4 - t, 516 - t))
+
     ts(V("t6", 0, 6), V("t6", 0, 6), V("pm", 0, 1), A.add)
-    ts(V("diagm", 0, NU), V("cmod", 0, NU), V("pm", 0, 1), A.is_equal)
+    quant(V("r16", 0, 128), V("tr16", 0, 512))
+    etile("e25", 0)
     quant(V("xq0", 0, 128), V("xt0", 0, 512))
     lay(V("sel", 96, 128), V("xq0", 96, 128))
     lay(V("selm", 0, 32), V("xq0", 96, 128))
@@ -311,14 +313,16 @@ def rank_program(g, core, T, topo):
         score(0, ps, u, v)
 
     units(*PIECES[0])
-    quant(V("r16", 0, 128), V("tr16", 0, 512))
-    run_max(*PIECES[0])
-    etile("e75", 0)
+    etile("e25", 1)
     units(*PIECES[1])
-    etile("e75", 1)
+    etile("e25", 2)
+    run_max(*PIECES[0])
+    etile("e25", 3)
     run_max(*PIECES[1])
     units(*PIECES[2])
+    etile("e75", 0)
     quant(V("negw", 0, 128), V("tnegw", 0, 512))
+    etile("e75", 1)
     run_max(*PIECES[2])
 
     for b in range(NR):
@@ -336,6 +340,8 @@ def rank_program(g, core, T, topo):
         reduce(V("h1", 0, 1), V("zz", 0, 24), A.add)
         ts(V("mbh", 0, XL), V("mb", 0, XL), V("h1", 0, 1), A.subtract)
         ts(V("xtile", 1, 4 * XL, 4), V("mask", 0, XL), V("h1", 0, 1), A.mult, 192.0, A.min)
+        if b == 0:
+            memset(V("xt1", 384, 512), 0.0)
         _record(rec, "scalar", "comp", lambda q: q.activation(T.xtile[:, 2:4 * XL:4], T.mb2[:, 0:XL], AF.Relu, bias=T.h1[:, 0:1]),
                 [V("mb2", 0, XL), V("h1", 0, 1)], [V("xtile", 2, 4 * XL, 4)])
         ts(V("xtile", 0, 4 * XL, 4), V("mbh", 0, XL), V(win, 0, 1), A.add, 0.0, A.max)
@@ -359,12 +365,12 @@ def rank_program(g, core, T, topo):
         quant(V("xf", 0, 128), V("xtile", 0, 512))
         mm(7, V("r16", 0, 128), V("xf", 0, 128))
         for t in range(3):
-            copy(V("nt", t, 512, 4), V("ps%d" % t, 0, 128), "scalar")
+            copy(V("nt", t, 4 * NT, 4), V("ps%d" % t, 0, NT), "scalar")
         if b == 1:
             copy(V("fsend", 0, 4), V("ps7", XL + 6, XL + 10), "scalar")
             send(partner, V("fland", 0, 4), V("fsend", 0, 4), "af1", "lf")
             tt(V("mval", 0, NT), V("diagm", 0, NU), V("jown", 0, NT), A.mult, off=lown)
-        copy(V("nt", 3, 512, 4), V("ps3", 0, 128))
+        copy(V("nt", 3, 4 * NT, 4), V("ps3", 0, NT))
         quant(V(tab, OWN, OWN + 128), V("nt", 0, 512))
         for x in (tab, tab + "s"):
             send(partner, V(x, PAR, PAR + NT), V(x, OWN, OWN + NT), "ac%d" % b, "lc")
@@ -372,6 +378,7 @@ def rank_program(g, core, T, topo):
             ts(V(lx[0], k, k + 1), V("d6", k, k + 1), V("ps7", XL + k, XL + k + 1), A.mult, V("t6", k, k + 1), A.add)
         if b == 0:
             send(partner, lxp, lx, "af0", "lf")
+            copy(V("src1", 0, NU), V("src0", 0, NU), "scalar")
             copy(V("ze50", 0, 520), V("z1", 0, 520), "scalar", scale=0.5)
             copy(V("reset", 0, NU), V("cmod", 0, NU), "scalar", func=AF.Sign)
         store("sync", T.ch[b:b + 1, 0:NT], V(win, 0, 1), T[win][0:NT, 0:1])
@@ -385,8 +392,7 @@ def rank_program(g, core, T, topo):
             copy(V("t6s", 3, 6), V("t6", 3, 6), "scalar", scale=-0.0625)
             for t in range(4):
                 etile("e50", t)
-            tt(V("src0", 0, NU), V("iotac", 0, NU), V("diagm", 0, NU), A.mult)
-            copy(V("src1", 0, NU), V("src0", 0, NU), "scalar")
+        scatter(V(src, 0, 480), lx, V("mval", 0, NT))
         arrive([land], "al%d" % b, partner)
         arrive([V(tab, PAR, PAR + NT), V(tab + "s", PAR, PAR + NT)], "ac%d" % b, partner, 2)
         arrive([lxp] if b == 0 else [V("fland", 0, 4)], "af%d" % b, partner)
@@ -396,24 +402,20 @@ def rank_program(g, core, T, topo):
         if b == 0:
             tt(*value)
         else:
-            scatter(V(src, 0, 480), lx, V("mval", 0, NT))
+            copy(V("lpf", 0, 3), V(land[0], 0, 3))
+            ts(V("lpf", 3, 6), V(land[0], 3, 6), -0.0625, A.mult)
         scan(V("c2", 0, NT), V("reset", 0, NT), V("c1", 0, NT), 0.0, A.mult, A.add)
         if b == 0:
             tt(*masked)
         else:
-            copy(V("lpf", 0, 3), V(land[0], 0, 3))
-            ts(V("lpf", 3, 6), V(land[0], 3, 6), -0.0625, A.mult)
-        copy(V("clist", 0, 6), V("c2", 15, NT, 16))
-        if b == 1:
             tt(V("d6p", 0, 6), V("lpf", 0, 6), V("t6s", 0, 6), A.subtract)
+        copy(V("clist", 0, 6), V("c2", 15, NT, 16))
         pick(V("selm", 32, 128), V(tab, 0, PAR), V("clist", 0, 6))
         own, par = V("selm", 0, 128), V(tab, PAR - 32, PAR + NT)
         for k, x in enumerate((par, own) if b == 0 else (own, par)):
             for t in range(4):
                 mm(t, V("e50", 128 * t, 128 * t + 128), x, k == 0, k == 1)
-        if b == 0:
-            scatter(V(src, 0, 480), lx, V("mval", 0, NT))
-        else:
+        if b == 1:
             tt(*value)
             ts(V("fb", 3, 6), V("fland", 0, 3), 8.0, A.is_ge, -16.0, A.mult)
             tt(*masked)
@@ -421,12 +423,12 @@ def rank_program(g, core, T, topo):
             for k in (3, 4, 5, 0, 1, 2):
                 ts(V(lxp[0], k, k + 1), V("d6p", k, k + 1), V("fb", k, k + 1), A.mult, V("t6", k, k + 1), A.add)
         scatter(V(src, 0, 480), lxp, V("pval", 0, NT))
-        scan(V("srcs", 0, NU), V("reset", 0, NU), V(src, 0, NU), 0.0, A.mult, A.add)
-        copy(V("blist", 0, 24), V("srcs", 15, NU, 16))
         if b == 0:
             quant(V("xq1", 0, 128), V("xt1", 0, 512))
+        scan(V("srcs", 0, NU), V("reset", 0, NU), V(src, 0, NU), 0.0, A.mult, A.add)
+        copy(V("blist", 0, 24), V("srcs", 15, NU, 16))
         for t in range(4):
-            copy(V("mt", t, 512, 4), V("ps%d" % t, 0, 128), "scalar")
+            copy(V("mt", 128 + t, 512, 4), V("ps%d" % t, 32, 128), "scalar")
         quant(V(tab, MQ, MQ + 128), V("mt", 0, 512))
         for ps, u, v in PIECES:
             pick(V(nxt, u, v), V(tab, 0, WIN), V("blist", u // 16, v // 16))

@@ -6,6 +6,7 @@ NU, NT, NR = 384, 96, 2
 OWN, PAR, MRG, WIN = 384, 512, 640, 736
 MQ = 608
 XC, XL = 128, 102
+BIG = 16384.0
 PIECES = ((4, 0, 128), (5, 128, 256), (6, 256, NU))
 F4, F32, BF, U16, I32, U8 = "float8_e4m3fn_x4", "float32", "bfloat16", "uint16", "int32", "uint8"
 
@@ -23,14 +24,12 @@ def _decl():
         pair("tab%d" % b, WIN)
         pair("xq%d" % b, 128)
         add("xt%d" % b, 512, BF)
-        for n in ("lown", "land", "lx", "lxp"):
+        for n in ("lown", "lx", "land"):
             add("%s%d" % (n, b), 6, U16)
-        add("mslot%d" % b, 480, F32)
         add("src%d" % b, 480, F32)
         add("win%d" % b, 1, F32)
-    for n in ("e25", "e75", "e50"):
+    for n in ("e25", "e75"):
         pair(n, 512)
-        add("z" + n, 520, BF)
     for n in ("r16", "r1", "negw"):
         pair(n, 128)
         add("t" + n, 512, BF)
@@ -39,22 +38,22 @@ def _decl():
     pair("fin", NU)
     for n in range(8):
         add("ps%d" % n, 512, F32, "psum")
-    for n, w, t in (("kbt", 1536, BF), ("wt", 512, BF), ("nt", 512, BF), ("mt", 512, BF), ("xtile", 4 * XC, BF), ("ones", 520, BF),
-                    ("fsend", 4, BF), ("fland", 4, BF), ("z1", 520, BF), ("mask", XL, BF), ("mask36", 36, BF), ("eq16", 128, BF),
-                    ("junk", NU, BF), ("mb", XL, BF), ("mbh", XL, BF), ("mb2", XL, BF), ("ip", 1, I32), ("pmi", 1, I32), ("pdi", 1, I32),
-                    ("clist", 6, U16), ("blist", 24, U16)):
+    for n, w, t in (("kbt", 1536, BF), ("wt", 512, BF), ("nt", 512, BF), ("mt", 512, BF), ("xtile", 4 * XC, BF), ("ones", 128, BF),
+                    ("ident", 128, BF), ("ze", 520, BF), ("mask", XL, BF), ("junk", NU, BF), ("mb", XL, BF), ("mbh", XL, BF),
+                    ("mb2", XL, BF), ("negc", 128, BF), ("cmod", 128, BF), ("iotac", 128, BF), ("eq16", 128, BF), ("ma", 128, BF),
+                    ("mc", 128, BF), ("mw", NU, BF), ("m6", 6, BF), ("cdig", 24, BF), ("pre", 24, BF),
+                    ("ip", 1, I32), ("pmi", 1, I32), ("pdi", 1, I32), ("clist", 6, U16), ("early", 6, U16), ("blist", 24, U16)):
         add(n, w, t)
-    for n, w in (("iotac", NU), ("cmod", NU), ("jown", NT), ("jpar", NT), ("t6", 6), ("t6s", 6), ("pcol", 1), ("pm", 1),
-                 ("pd", 1), ("negc", 128), ("diagm", NU), ("reset", NU), ("p", NU), ("zz", 24), ("h1", 1), ("dmin", 1),
-                 ("d6", 6), ("mval", NT), ("mf1", NU), ("mflag", NU), ("c1", NT), ("c2", NT), ("val", NT),
-                 ("pval", NT), ("lpf", 6), ("d6p", 6), ("fb", 6), ("srcs", NU), ("ysb", NU)):
+    for n, w in (("jown", NT), ("jpar", NT), ("pcol", 1), ("pm", 1), ("pm1", 1), ("pd", 1), ("p", NU), ("zz", 24), ("h1", 1),
+                 ("dmin", 1), ("flag", 1), ("q6", 1), ("cf", 1), ("esc0", 1), ("esc", 1), ("c1", NT), ("c2", NT), ("sg", NT),
+                 ("both", NT), ("val", NT), ("srcs", NU), ("ysb", NU)):
         add(n, w, F32)
     return s
 
 
 SCRATCH = _decl()
 NCOMP, NHW = 90, 30
-REMOTE = ["%s%d" % (n, b) for b in range(NR) for n in ("al", "ac", "af")] + ["ll", "lc", "lf"]
+REMOTE = ["%s%d" % (n, b) for b in range(NR) for n in ("al", "ac")] + ["ae0", "ll", "lc"]
 SEMAPHORES = ["c%d" % i for i in range(NCOMP)] + ["h%d" % i for i in range(NHW)] + REMOTE
 
 
@@ -154,17 +153,18 @@ def rank_program(g, core, T, topo):
     def memset(out, c):
         _record(rec, "vector", "comp", lambda q: q.memset(ap(out), c), [], [out])
 
-    def copy(out, in_, queue="vector", scale=None, bias=None, func=None):
+    def copy(out, in_, queue="vector", scale=None, bias=None, off=None, func=None):
+        src = (lambda: ap(in_)) if off is None else (lambda: ap(in_).indirect(ap(off)))
         if queue == "vector":
-            _record(rec, "vector", "comp", lambda q: q.tensor_copy(ap(out), ap(in_)), [in_], [out])
+            _record(rec, "vector", "comp", lambda q: q.tensor_copy(ap(out), src()), views(in_, off), [out])
             return
         f = func or (AF.Copy if bias is None else AF.Identity)
         kw = {}
         if scale is not None:
-            kw["scale"] = scale
+            kw["scale"] = val(scale)
         if bias is not None:
             kw["bias"] = bias
-        _record(rec, "scalar", "comp", lambda q: q.activation(ap(out), ap(in_), f, **kw), [in_], [out])
+        _record(rec, "scalar", "comp", lambda q: q.activation(ap(out), src(), f, **kw), views(in_, scale, off), [out])
 
     def ts(out, in0, s1, op0, s2=None, op1=None):
         def call(q):
@@ -173,11 +173,8 @@ def rank_program(g, core, T, topo):
             return q.tensor_scalar(ap(out), ap(in0), val(s1), val(s2), op0, op1)
         _record(rec, "vector", "comp", call, views(in0, s1, s2), [out])
 
-    def tt(out, in0, in1, op, off=None):
-        def call(q):
-            i0 = ap(in0) if off is None else ap(in0).indirect(ap(off))
-            return q.tensor_tensor(ap(out), i0, ap(in1), op)
-        _record(rec, "vector", "comp", call, views(in0, in1, off), [out])
+    def tt(out, in0, in1, op):
+        _record(rec, "vector", "comp", lambda q: q.tensor_tensor(ap(out), ap(in0), ap(in1), op), [in0, in1], [out])
 
     def scatter(win, off, in_):
         _record(rec, "vector", "comp", lambda q: q.tensor_copy(ap(win).indirect(ap(off)), ap(in_)), [win, off, in_], [win])
@@ -249,53 +246,49 @@ def rank_program(g, core, T, topo):
     kb2 = load("sync", V("kbt", 1024, 1536), T.kb[:, 1024:1536])
 
     iota(V("ip", 0, 1), [[0, 1]], 0, 1)
-    iota(V("cmod", 0, NU), [[0, 24], [1, 16]], 0, 0)
+    memset(V("ones", 0, 128), 1.0)
+    _record(rec, "gpsimd", "comp", lambda q: q.affine_select(T.ident[:, 0:128], T.ones[:, 0:128], [[-1, 128]], A.is_equal, 0.0, 0, 1),
+            [V("ones", 0, 128)], [V("ident", 0, 128)])
+    iota(V("cmod", 0, 128), [[0, 8], [1, 16]], 0, 0)
     iota(V("pcol", 0, 1), [[0, 1]], 0, 1)
-    iota(V("iotac", 0, NU), [[1, NU]], 0, 0)
-    memset(V("ones", 0, 520), 1.0)
-    _record(rec, "gpsimd", "comp", lambda q: q.affine_select(T.z1[:, 0:520], T.ones[:, 0:520], [[-1, 520]], A.is_equal, 0.0, 4, 4),
-            [V("ones", 0, 520)], [V("z1", 0, 520)])
-    iota(V("t6", 0, 6), [[16, 6]], NU, 0)
+    iota(V("iotac", 0, 128), [[1, 128]], 0, 0)
     iota(V("jown", 0, NT), [[1, NT]], OWN, 0)
-    iota(V("jpar", 0, NT), [[1, NT]], PAR, 0)
-    ts(V("pmi", 0, 1), V("ip", 0, 1), 15, A.bitwise_and)
-    ts(V("pdi", 0, 1), V("ip", 0, 1), 4, A.logical_shift_right)
-    copy(V("pm", 0, 1), V("pmi", 0, 1))
-    copy(V("pd", 0, 1), V("pdi", 0, 1))
-    memset(V("xtile", 0, 4 * XC), 0.0)
-    memset(V("mask36", 0, 36), 0.0)
-    ts(V("eq16", 0, 128), V("cmod", 0, 128), V("pm", 0, 1), A.is_equal)
-    ts(V("diagm", 0, NU), V("cmod", 0, NU), V("pm", 0, 1), A.is_equal)
-    memset(V("tr1", 0, 512), 1.0)
-    ts(V("mask", 0, NT), V("iotac", 0, NT), V("pcol", 0, 1), A.is_equal)
-    ts(V("mask", NT, XL), V("iotac", 0, 6), V("pd", 0, 1), A.is_equal)
-    ts(V("tr1", 3, 512, 4), V("iotac", 0, 128), V("pcol", 0, 1), A.is_le, 512.0, A.mult)
+    iota(V("src0", 0, 480), [[1, 480]], 0, 0)
+    iota(V("jpar", 0, NT), [[1, NT]], (PAR + MRG) // 2, 0)
+    iota(V("src1", 0, 480), [[1, 480]], 0, 0)
+    for c in range(0, 520, 128):
+        n = min(128, 520 - c)
+        copy(V("ze", c, c + n), V("ones", 0, n), "scalar", scale=0.0)
+    copy(V("ze", 4, 516, 4), V("ident", 0, 128), "scalar", scale=0.25)
     memset(V("xt0", 384, 512), 0.0)
     memset(V("negc", 0, 128), -1e29)
-    tt(V("src0", 0, NU), V("iotac", 0, NU), V("diagm", 0, NU), A.mult)
-    quant(V("r1", 0, 128), V("tr1", 0, 512))
-    for t in range(4):
-        copy(V("tr16", t, 512, 4), V("eq16", 0, 128), "scalar", scale=16.0 if t == 3 else 1.0)
-    copy(V("xtile", 3, 4 * NT, 4), V("mask", 0, NT), "scalar")
-    for n, c in (("e25", 0.25), ("e75", 0.75)):
-        copy(V("z" + n, 0, 520), V("z1", 0, 520), "scalar", scale=c)
-    for t in range(4):
-        copy(V("tnegw", t, 512, 4), V("eq16", 0, 128), "scalar", scale=0.0, bias=0.0 if t == 3 else -1.0)
-    copy(V("mb", 0, XL), V("mask", 0, XL), "scalar", scale=1024.0, bias=-1024.0)
-    copy(V("mb2", 0, XL), V("mask", 0, XL), "scalar", scale=1024.0, bias=-1024.0 - 192.0)
-    copy(V("mask36", 0, 24, 4), V("mask", NT, XL), "scalar")
-    copy(V("mask36", 24, 36, 4), V("mask", NT, NT + 3), "scalar")
-    copy(V("mask36", 27, 36, 4), V("mask", NT + 3, XL), "scalar")
-    for n, c in (("nt", 4 * NT), ("mt", 0)):
-        copy(V(n, c, c + 128), V("eq16", 0, 128), "scalar", scale=0.0)
-    copy(V("mslot0", 0, NU), V("iotac", 0, NU), "scalar", scale=0.0)
+    ts(V("pmi", 0, 1), V("ip", 0, 1), 15, A.bitwise_and)
+    ts(V("pdi", 0, 1), V("ip", 0, 1), 4, A.logical_shift_right)
+    memset(V("xtile", 4 * XL, 4 * XC), 0.0)
+    copy(V("pm", 0, 1), V("pmi", 0, 1))
+    copy(V("pd", 0, 1), V("pdi", 0, 1))
+    memset(V("xtile", 4 * NT + 3, 4 * XL, 4), 0.0)
+    memset(V("tnegw", 0, 512), -1.0)
+    copy(V("xtile", 3, 4 * NT, 4), V("ident", 0, NT), "scalar")
+    copy(V("mask", 0, NT), V("ident", 0, NT), "scalar")
 
     def etile(n, t):
-        quant(V(n, 128 * t, 128 * t + 128), V("z" + n, 4 - t, 516 - t))
+        quant(V(n, 128 * t, 128 * t + 128), V("ze", 4 - t, 516 - t))
 
-    ts(V("t6", 0, 6), V("t6", 0, 6), V("pm", 0, 1), A.add)
-    quant(V("r16", 0, 128), V("tr16", 0, 512))
     etile("e25", 0)
+    ts(V("eq16", 0, 128), V("cmod", 0, 128), V("pm", 0, 1), A.is_equal)
+    for t in range(4):
+        copy(V("tr16", t, 512, 4), V("eq16", 0, 128), "scalar", scale=16.0 if t == 3 else 1.0)
+    etile("e25", 1)
+    etile("e25", 2)
+    memset(V("tnegw", 3, 512, 4), 0.0)
+    etile("e25", 3)
+    copy(V("ze", 4, 516, 4), V("ident", 0, 128), "scalar", scale=0.75)
+    for t in range(3):
+        copy(V("tr1", t, 512, 4), V("eq16", 0, 128), "scalar", scale=0.0, bias=1.0)
+    ts(V("mask", NT, XL), V("iotac", 0, 6), V("pd", 0, 1), A.is_equal)
+    copy(V("mb", 0, XL), V("mask", 0, XL), "scalar", scale=1024.0, bias=-1024.0)
+    copy(V("mb2", 0, XL), V("mask", 0, XL), "scalar", scale=1024.0, bias=-1024.0 - 192.0)
     quant(V("xq0", 0, 128), V("xt0", 0, 512))
     lay(V("sel", 96, 128), V("xq0", 96, 128))
     lay(V("selm", 0, 32), V("xq0", 96, 128))
@@ -308,27 +301,21 @@ def rank_program(g, core, T, topo):
     def run_max(ps, u, v):
         scan(V("p", u, v), V("ps%d" % ps, 0, v - u), V("negc", 0, v - u), V("p", u - 1, u) if u else -1e29, A.max, A.max)
 
-    def units(ps, u, v):
+    for ps, u, v in PIECES:
         quant(V("tab0", u, v), V("kbt", 4 * u, 4 * v))
         score(0, ps, u, v)
-
-    units(*PIECES[0])
-    etile("e25", 1)
-    units(*PIECES[1])
-    etile("e25", 2)
+    ts(V("tr1", 3, 512, 4), V("iotac", 0, 128), V("pcol", 0, 1), A.is_le, 512.0, A.mult)
+    quant(V("r16", 0, 128), V("tr16", 0, 512))
     run_max(*PIECES[0])
-    etile("e25", 3)
-    run_max(*PIECES[1])
-    units(*PIECES[2])
-    etile("e75", 0)
     quant(V("negw", 0, 128), V("tnegw", 0, 512))
-    etile("e75", 1)
+    run_max(*PIECES[1])
+    quant(V("r1", 0, 128), V("tr1", 0, 512))
     run_max(*PIECES[2])
 
     for b in range(NR):
         tab, xq, nxt = "tab%d" % b, "xq%d" % b, "tab%d" % (b + 1) if b + 1 < NR else "fin"
-        win, mslot, src = "win%d" % b, "mslot%d" % b, "src%d" % b
-        lown, land, lx, lxp = [V("%s%d" % (n, b), 0, 6) for n in ("lown", "land", "lx", "lxp")]
+        win, src = "win%d" % b, V("src%d" % b, 0, 480)
+        lown, lx, land = [V("%s%d" % (n, b), 0, 6) for n in ("lown", "lx", "land")]
         partner = T.cores[rank ^ (1 << b)]
         for t in range(4):
             mm(t, V("e25", 128 * t, 128 * t + 128), V(xq, 0, 128), True, False)
@@ -337,98 +324,101 @@ def rank_program(g, core, T, topo):
                 lambda q, w=win: q.activation(T.junk[:, 0:NU], T.p[:, 0:NU], AF.Sign, bias=T.p[:, NU - 1:NU], scale=-1.0,
                                               accum_out=T[w][:, 0:1]), [V("p", 0, NU)], [V("junk", 0, NU), V(win, 0, 1)])
         ts(V("zz", 0, 24), V("p", 15, NU, 16), last, A.is_lt, 16.0, A.mult)
+        if b == 0:
+            ts(V("q6", 0, 1), V("pd", 0, 1), 6.0, A.is_equal)
         reduce(V("h1", 0, 1), V("zz", 0, 24), A.add)
+        if b == 0:
+            ts(V("cf", 0, 1), V("pd", 0, 1), 6.0, A.is_ge)
         ts(V("mbh", 0, XL), V("mb", 0, XL), V("h1", 0, 1), A.subtract)
         ts(V("xtile", 1, 4 * XL, 4), V("mask", 0, XL), V("h1", 0, 1), A.mult, 192.0, A.min)
         if b == 0:
-            memset(V("xt1", 384, 512), 0.0)
+            ts(V("m6", 0, 6), V("mask", NT, XL), V("q6", 0, 1), A.subtract)
+            ts(V("pm1", 0, 1), V("pm", 0, 1), 1.0, A.add)
+            tt(V("cdig", 3, 24, 4), V("m6", 0, 6), V("iotac", 0, 6), A.mult)
+            etile("e75", 0)
         _record(rec, "scalar", "comp", lambda q: q.activation(T.xtile[:, 2:4 * XL:4], T.mb2[:, 0:XL], AF.Relu, bias=T.h1[:, 0:1]),
                 [V("mb2", 0, XL), V("h1", 0, 1)], [V("xtile", 2, 4 * XL, 4)])
         ts(V("xtile", 0, 4 * XL, 4), V("mbh", 0, XL), V(win, 0, 1), A.add, 0.0, A.max)
         quant(V("xl", 0, XC), V("xtile", 0, 4 * XC))
-        if b == 0:
-            etile("e75", 2)
-            etile("e75", 3)
-        else:
-            quant(V("wq", 0, 128), V("wt", 0, 512))
         mm(5, V("r16", 0, 128), V("xl", 0, XC))
         mm(6, V("r1", 0, 128), V("xl", 0, XC), True, False)
         mm(6, V("xl", 0, XC), V("negw", 0, 128), False, True)
+        if b == 0:
+            copy(V("cdig", 0, 24, 4), V("m6", 0, 6), "scalar", scale=V("pm", 0, 1))
+            copy(V("cdig", 1, 24, 4), V("m6", 0, 6), "scalar", scale=192.0)
+            copy(V("cdig", 2, 24, 4), V("m6", 0, 6), "scalar", scale=192.0)
+            etile("e75", 1)
+            etile("e75", 2)
+        else:
+            tt(V("pre", 0, 24), V("xtile", 4 * NT, 4 * XL), V("cdig", 0, 24), A.subtract)
         copy(lown, V("ps5", NT, XL))
-        send(partner, land, lown, "al%d" % b, "ll")
+        if b == 0:
+            send(partner, V("early", 0, 6), lown, "ae0", "ll")
         pick(V("sel", 0, NT), V(tab, 0, NU), lown)
+        if b == 0:
+            etile("e75", 3)
+            tt(V("pre", 0, 24), V("xtile", 4 * NT, 4 * XL), V("cdig", 0, 24), A.subtract)
         for t in range(4):
             mm(t, V("e75", 128 * t, 128 * t + 128), V("sel", 0, 128), False, True)
         reduce(V("dmin", 0, 1), V("ps6", 0, NT), A.min, absv=True)
-        tt(V("d6", 0, 6), V("ps5", NT, XL), V("t6", 0, 6), A.subtract)
-        ts(V("xtile", 4 * XL, 4 * XL + 36), V("mask36", 0, 36), V("dmin", 0, 1), A.mult, 1.0, A.min)
+        if b == 0:
+            ts(V("esc0", 0, 1), V("pm", 0, 1), 15.0, A.is_ge, 1.0 - 1.0 / BIG, A.mult)
+        ts(V("flag", 0, 1), V("dmin", 0, 1), 1.0, A.min, V("cf", 0, 1), A.max)
+        if b == 0:
+            ts(V("esc", 0, 1), V("esc0", 0, 1), 1.0 / BIG, A.add)
+        ts(V("xtile", 4 * XL, 4 * XL + 24), V("pre", 0, 24), V("flag", 0, 1), A.mult)
+        if b == 0:
+            for n, c in (("nt", 4 * NT), ("mt", 0)):
+                copy(V(n, c, c + 128), V("eq16", 0, 128), "scalar", scale=0.0)
+            ts(V("ma", 0, 128), V("cmod", 0, 128), V("pm", 0, 1), A.not_equal)
+            ts(V("mc", 0, 128), V("cmod", 0, 128), V("pm1", 0, 1), A.is_equal, BIG, A.mult)
         quant(V("xf", 0, 128), V("xtile", 0, 512))
         mm(7, V("r16", 0, 128), V("xf", 0, 128))
         for t in range(3):
             copy(V("nt", t, 4 * NT, 4), V("ps%d" % t, 0, NT), "scalar")
         if b == 1:
-            copy(V("fsend", 0, 4), V("ps7", XL + 6, XL + 10), "scalar")
-            send(partner, V("fland", 0, 4), V("fsend", 0, 4), "af1", "lf")
-            tt(V("mval", 0, NT), V("diagm", 0, NU), V("jown", 0, NT), A.mult, off=lown)
+            copy(lx, V("ps7", XL, XL + 6))
+            send(partner, land, lx, "al1", "ll")
         copy(V("nt", 3, 4 * NT, 4), V("ps3", 0, NT))
         quant(V(tab, OWN, OWN + 128), V("nt", 0, 512))
         for x in (tab, tab + "s"):
             send(partner, V(x, PAR, PAR + NT), V(x, OWN, OWN + NT), "ac%d" % b, "lc")
-        for k in range(6):
-            ts(V(lx[0], k, k + 1), V("d6", k, k + 1), V("ps7", XL + k, XL + k + 1), A.mult, V("t6", k, k + 1), A.add)
         if b == 0:
-            send(partner, lxp, lx, "af0", "lf")
-            copy(V("src1", 0, NU), V("src0", 0, NU), "scalar")
-            copy(V("ze50", 0, 520), V("z1", 0, 520), "scalar", scale=0.5)
-            copy(V("reset", 0, NU), V("cmod", 0, NU), "scalar", func=AF.Sign)
+            copy(lx, V("ps7", XL, XL + 6))
+            send(partner, land, lx, "al0", "ll")
         store("sync", T.ch[b:b + 1, 0:NT], V(win, 0, 1), T[win][0:NT, 0:1])
-        scatter(V(mslot, 0, 480), lx, V("jown", 0, NT))
-        copy(V("mf1", 0, NU), V(mslot, 0, NU), "scalar", func=AF.Sign)
-        copy(V("mflag", 0, NU), V("mf1", 0, NU), "scalar", scale=float(MRG - PAR))
         if b == 0:
-            tt(V("mval", 0, NT), V("diagm", 0, NU), V("jown", 0, NT), A.mult, off=lown)
-            copy(V("mslot1", 0, NU), V("iotac", 0, NU), "scalar", scale=0.0)
-            copy(V("t6s", 0, 3), V("t6", 0, 3), "scalar")
-            copy(V("t6s", 3, 6), V("t6", 3, 6), "scalar", scale=-0.0625)
-            for t in range(4):
-                etile("e50", t)
-        scatter(V(src, 0, 480), lx, V("mval", 0, NT))
+            tt(V("mw", 0, 128), V("ma", 0, 128), V("mc", 0, 128), A.max)
+            copy(V("mw", 128, 256), V("mw", 0, 128), "scalar")
+            copy(V("mw", 256, NU), V("mw", 0, 128), "scalar")
+        scatter(src, lx, V("jown", 0, NT))
+        if b == 1:
+            quant(V("wq", 0, 128), V("wt", 0, 512))
+        look = land
+        if b == 0:
+            look = V("early", 0, 6)
+            arrive([look], "ae0", partner)
         arrive([land], "al%d" % b, partner)
         arrive([V(tab, PAR, PAR + NT), V(tab + "s", PAR, PAR + NT)], "ac%d" % b, partner, 2)
-        arrive([lxp] if b == 0 else [V("fland", 0, 4)], "af%d" % b, partner)
-        value = (V("val", 0, NT), V("mflag", 0, NU), V("jpar", 0, NT), A.add, land)
-        masked = (V("pval", 0, NT), V("diagm", 0, NU), V("val", 0, NT), A.mult, land)
-        tt(V("c1", 0, NT), V(mslot, 0, NU), V("diagm", 0, NT), A.mult, land)
-        if b == 0:
-            tt(*value)
-        else:
-            copy(V("lpf", 0, 3), V(land[0], 0, 3))
-            ts(V("lpf", 3, 6), V(land[0], 3, 6), -0.0625, A.mult)
-        scan(V("c2", 0, NT), V("reset", 0, NT), V("c1", 0, NT), 0.0, A.mult, A.add)
-        if b == 0:
-            tt(*masked)
-        else:
-            tt(V("d6p", 0, 6), V("lpf", 0, 6), V("t6s", 0, 6), A.subtract)
-        copy(V("clist", 0, 6), V("c2", 15, NT, 16))
+        copy(V("c1", 0, NT), src, off=look)
+        copy(V("sg", 0, NT), src, "scalar", bias=0.5 - OWN, off=look, func=AF.Sign)
+        copy(V("both", 0, NT), V("sg", 0, NT), "scalar", scale=(MRG - PAR) / 2.0)
+        scan(V("c2", 0, NT), V("mw", 0, NT), V("c1", 0, NT), 0.0, A.mult, A.add)
+        ts(V("clist", 0, 6), V("c2", 15, NT, 16), V("esc", 0, 1), A.mult, -0.34, A.add)
+        tt(V("val", 0, NT), V("both", 0, NT), V("jpar", 0, NT), A.add)
         pick(V("selm", 32, 128), V(tab, 0, PAR), V("clist", 0, 6))
-        own, par = V("selm", 0, 128), V(tab, PAR - 32, PAR + NT)
-        for k, x in enumerate((par, own) if b == 0 else (own, par)):
+        parts = [V(tab, PAR - 32, PAR + NT), V("selm", 0, 128)]
+        for k, x in enumerate(parts[::-1] if b == 0 else parts):
             for t in range(4):
-                mm(t, V("e50", 128 * t, 128 * t + 128), x, k == 0, k == 1)
-        if b == 1:
-            tt(*value)
-            ts(V("fb", 3, 6), V("fland", 0, 3), 8.0, A.is_ge, -16.0, A.mult)
-            tt(*masked)
-            tt(V("fb", 0, 3), V("fland", 0, 3), V("fb", 3, 6), A.add)
-            for k in (3, 4, 5, 0, 1, 2):
-                ts(V(lxp[0], k, k + 1), V("d6p", k, k + 1), V("fb", k, k + 1), A.mult, V("t6", k, k + 1), A.add)
-        scatter(V(src, 0, 480), lxp, V("pval", 0, NT))
+                mm(t, V("e25", 128 * t, 128 * t + 128), x, k == 0, k == 1)
+        scatter(src, land, V("val", 0, NT))
+        scan(V("srcs", 0, NU), V("mw", 0, NU), V(src[0], 0, NU), 0.0, A.mult, A.add)
+        ts(V("blist", 0, 24), V("srcs", 15, NU, 16), V("esc", 0, 1), A.mult, -0.34, A.add)
         if b == 0:
+            memset(V("xt1", 384, 512), 0.0)
             quant(V("xq1", 0, 128), V("xt1", 0, 512))
-        scan(V("srcs", 0, NU), V("reset", 0, NU), V(src, 0, NU), 0.0, A.mult, A.add)
-        copy(V("blist", 0, 24), V("srcs", 15, NU, 16))
         for t in range(4):
-            copy(V("mt", 128 + t, 512, 4), V("ps%d" % t, 32, 128), "scalar")
+            copy(V("mt", 128 + t, 512, 4), V("ps%d" % t, 32, 128), "scalar", scale=2.0)
         quant(V(tab, MQ, MQ + 128), V("mt", 0, 512))
         for ps, u, v in PIECES:
             pick(V(nxt, u, v), V(tab, 0, WIN), V("blist", u // 16, v // 16))
@@ -448,7 +438,6 @@ def rank_program(g, core, T, topo):
         store("scalar", T.osc[4 * k:4 * k + 4, 0:NU], V("fins", 0, NU), T.fins[32 * k:32 * k + 4, 0:NU])
     _record(rec, "sync", "end", None, [], [], stores)
     _issue(rec, {"vector": g.vector, "scalar": g.scalar, "tensor": g.tensor, "gpsimd": g, "sync": g.sync}, T.sem)
-    n = sum(len(lanes(core, T.cores[rank ^ (1 << b)])) for b in range(NR))
-    g.wait_ge(T.sem.ll, n)
-    g.wait_ge(T.sem.lc, 2 * n)
-    g.wait_ge(T.sem.lf, n)
+    n = [len(lanes(core, T.cores[rank ^ (1 << b)])) for b in range(NR)]
+    g.wait_ge(T.sem.ll, 2 * n[0] + n[1])
+    g.wait_ge(T.sem.lc, 2 * n[0] + 2 * n[1])

@@ -23,8 +23,10 @@ def _decl():
     for b in range(NR):
         pair("tab%d" % b, WIN)
         pair("xq%d" % b, 128)
+        pair("xl%d" % b, 128)
+        pair("ex%d" % b, 128)
         add("xt%d" % b, 512, BF)
-        for n in ("lown", "lx", "land"):
+        for n in ("lown", "lx", "land", "look"):
             add("%s%d" % (n, b), 6, U16)
         add("src%d" % b, 480, F32)
         add("win%d" % b, 1, F32)
@@ -33,19 +35,19 @@ def _decl():
     for n in ("r16", "r1", "negw"):
         pair(n, 128)
         add("t" + n, 512, BF)
-    for n in ("sel", "selm", "xl", "xf", "wq"):
+    for n in ("sel", "selm", "xf", "wq"):
         pair(n, 128)
     pair("fin", NU)
     for n in range(8):
         add("ps%d" % n, 512, F32, "psum")
     for n, w, t in (("kbt", 1536, BF), ("wt", 512, BF), ("nt", 512, BF), ("mt", 512, BF), ("xtile", 4 * XC, BF), ("ones", 128, BF),
-                    ("ident", 128, BF), ("ze", 520, BF), ("mask", XL, BF), ("junk", NU, BF), ("mb", XL, BF), ("mbh", XL, BF),
-                    ("mb2", XL, BF), ("negc", 128, BF), ("cmod", 128, BF), ("iotac", 128, BF), ("eq16", 128, BF), ("ma", 128, BF),
-                    ("mc", 128, BF), ("mw", NU, BF), ("m6", 6, BF), ("cdig", 24, BF), ("pre", 24, BF),
-                    ("ip", 1, I32), ("pmi", 1, I32), ("pdi", 1, I32), ("clist", 6, U16), ("early", 6, U16), ("blist", 24, U16)):
+                    ("ident", 128, BF), ("ze", 520, BF), ("mask", XL + 1, BF), ("junk", NU, BF), ("mb", XL, BF), ("mbh", XL, BF),
+                    ("mb2", XL, BF), ("negc", 128, BF), ("cmod", 128, BF), ("iotac", 128, BF), ("eq16", 128, BF), ("ma", 16, BF),
+                    ("mc", 16, BF), ("mw", NU, BF), ("m6", 6, BF), ("cdig", 24, BF), ("pre", 24, BF),
+                    ("ip", 1, I32), ("pmi", 1, I32), ("pdi", 1, I32), ("clist", 6, U16), ("blist", 24, U16)):
         add(n, w, t)
-    for n, w in (("jown", NT), ("jpar", NT), ("pcol", 1), ("pm", 1), ("pm1", 1), ("pd", 1), ("p", NU), ("zz", 24), ("h1", 1),
-                 ("dmin", 1), ("flag", 1), ("q6", 1), ("cf", 1), ("esc0", 1), ("esc", 1), ("c1", NT), ("c2", NT), ("sg", NT),
+    for n, w in (("jown", NT), ("jpar", NT), ("pcol", 1), ("pm", 1), ("pd", 1), ("p", NU), ("zz", 24), ("h1", 1),
+                 ("dmin", 1), ("flag", 1), ("cf", 1), ("esc0", 1), ("esc", 1), ("c1", NT), ("c2", NT), ("sg", NT),
                  ("both", NT), ("val", NT), ("srcs", NU), ("ysb", NU)):
         add(n, w, F32)
     return s
@@ -53,7 +55,7 @@ def _decl():
 
 SCRATCH = _decl()
 NCOMP, NHW = 90, 30
-REMOTE = ["%s%d" % (n, b) for b in range(NR) for n in ("al", "ac")] + ["ae0", "ll", "lc"]
+REMOTE = ["%s%d" % (n, b) for b in range(NR) for n in ("ae", "al", "ac")] + ["le", "ll", "lc"]
 SEMAPHORES = ["c%d" % i for i in range(NCOMP)] + ["h%d" % i for i in range(NHW)] + REMOTE
 
 
@@ -256,9 +258,7 @@ def rank_program(g, core, T, topo):
     iota(V("src0", 0, 480), [[1, 480]], 0, 0)
     iota(V("jpar", 0, NT), [[1, NT]], (PAR + MRG) // 2, 0)
     iota(V("src1", 0, 480), [[1, 480]], 0, 0)
-    for c in range(0, 520, 128):
-        n = min(128, 520 - c)
-        copy(V("ze", c, c + n), V("ones", 0, n), "scalar", scale=0.0)
+    memset(V("ze", 0, 520), 0.0)
     copy(V("ze", 4, 516, 4), V("ident", 0, 128), "scalar", scale=0.25)
     memset(V("xt0", 384, 512), 0.0)
     memset(V("negc", 0, 128), -1e29)
@@ -268,32 +268,11 @@ def rank_program(g, core, T, topo):
     copy(V("pm", 0, 1), V("pmi", 0, 1))
     copy(V("pd", 0, 1), V("pdi", 0, 1))
     memset(V("xtile", 4 * NT + 3, 4 * XL, 4), 0.0)
-    memset(V("tnegw", 0, 512), -1.0)
     copy(V("xtile", 3, 4 * NT, 4), V("ident", 0, NT), "scalar")
     copy(V("mask", 0, NT), V("ident", 0, NT), "scalar")
 
     def etile(n, t):
         quant(V(n, 128 * t, 128 * t + 128), V("ze", 4 - t, 516 - t))
-
-    etile("e25", 0)
-    ts(V("eq16", 0, 128), V("cmod", 0, 128), V("pm", 0, 1), A.is_equal)
-    for t in range(4):
-        copy(V("tr16", t, 512, 4), V("eq16", 0, 128), "scalar", scale=16.0 if t == 3 else 1.0)
-    etile("e25", 1)
-    etile("e25", 2)
-    memset(V("tnegw", 3, 512, 4), 0.0)
-    etile("e25", 3)
-    copy(V("ze", 4, 516, 4), V("ident", 0, 128), "scalar", scale=0.75)
-    for t in range(3):
-        copy(V("tr1", t, 512, 4), V("eq16", 0, 128), "scalar", scale=0.0, bias=1.0)
-    ts(V("mask", NT, XL), V("iotac", 0, 6), V("pd", 0, 1), A.is_equal)
-    copy(V("mb", 0, XL), V("mask", 0, XL), "scalar", scale=1024.0, bias=-1024.0)
-    copy(V("mb2", 0, XL), V("mask", 0, XL), "scalar", scale=1024.0, bias=-1024.0 - 192.0)
-    quant(V("xq0", 0, 128), V("xt0", 0, 512))
-    lay(V("sel", 96, 128), V("xq0", 96, 128))
-    lay(V("selm", 0, 32), V("xq0", 96, 128))
-    load("sync", V("xt1", 0, 384), T.x[:, 384:768], [kb2])
-    load("sync", V("wt", 0, 512), T.w[:, 0:512], [kb2])
 
     def score(b, ps, u, v):
         mm(ps, V("xq%d" % b, 0, 128), V("tab%d" % b, u, v))
@@ -301,122 +280,147 @@ def rank_program(g, core, T, topo):
     def run_max(ps, u, v):
         scan(V("p", u, v), V("ps%d" % ps, 0, v - u), V("negc", 0, v - u), V("p", u - 1, u) if u else -1e29, A.max, A.max)
 
-    for ps, u, v in PIECES:
+    def units(ps, u, v):
         quant(V("tab0", u, v), V("kbt", 4 * u, 4 * v))
         score(0, ps, u, v)
-    ts(V("tr1", 3, 512, 4), V("iotac", 0, 128), V("pcol", 0, 1), A.is_le, 512.0, A.mult)
-    quant(V("r16", 0, 128), V("tr16", 0, 512))
+
+    quant(V("xq0", 0, 128), V("xt0", 0, 512))
+    lay(V("sel", 96, 128), V("xq0", 96, 128))
+    lay(V("selm", 0, 32), V("xq0", 96, 128))
+    for b in range(NR):
+        lay(V("ex%d" % b, 6, 128), V("xq0", 0, 122))
+    load("sync", V("xt1", 0, 384), T.x[:, 384:768], [kb2])
+    load("sync", V("wt", 0, 512), T.w[:, 0:512], [kb2])
+    etile("e25", 0)
+    units(*PIECES[0])
+    etile("e25", 1)
+    units(*PIECES[1])
+    ts(V("eq16", 0, 128), V("cmod", 0, 128), V("pm", 0, 1), A.is_equal)
+    for t in range(4):
+        copy(V("tr16", t, 512, 4), V("eq16", 0, 128), "scalar", scale=16.0 if t == 3 else 1.0)
     run_max(*PIECES[0])
-    quant(V("negw", 0, 128), V("tnegw", 0, 512))
+    units(*PIECES[2])
+    ts(V("mask", NT, XL + 1), V("iotac", 0, 7), V("pd", 0, 1), A.is_equal)
+    copy(V("mb", 0, XL), V("mask", 0, XL), "scalar", scale=1024.0, bias=-1024.0)
+    copy(V("mb2", 0, XL), V("mask", 0, XL), "scalar", scale=1024.0, bias=-1024.0 - 192.0)
     run_max(*PIECES[1])
-    quant(V("r1", 0, 128), V("tr1", 0, 512))
+    memset(V("tnegw", 0, 512), -1.0)
     run_max(*PIECES[2])
+    memset(V("tnegw", 3, 512, 4), 0.0)
+    etile("e25", 2)
 
     for b in range(NR):
         tab, xq, nxt = "tab%d" % b, "xq%d" % b, "tab%d" % (b + 1) if b + 1 < NR else "fin"
         win, src = "win%d" % b, V("src%d" % b, 0, 480)
-        lown, lx, land = [V("%s%d" % (n, b), 0, 6) for n in ("lown", "lx", "land")]
+        lown, lx, land, look = [V("%s%d" % (n, b), 0, 6) for n in ("lown", "lx", "land", "look")]
+        xl, ex = V("xl%d" % b, 0, XC), V("ex%d" % b, 0, 128)
         partner = T.cores[rank ^ (1 << b)]
-        for t in range(4):
-            mm(t, V("e25", 128 * t, 128 * t + 128), V(xq, 0, 128), True, False)
+
+        def tokens(xq=xq):
+            for t in range(4):
+                mm(t, V("e25", 128 * t, 128 * t + 128), V(xq, 0, 128), True, False)
+
+        if b == 1:
+            tokens()
         last = V("p", NU - 1, NU)
         _record(rec, "scalar", "comp",
                 lambda q, w=win: q.activation(T.junk[:, 0:NU], T.p[:, 0:NU], AF.Sign, bias=T.p[:, NU - 1:NU], scale=-1.0,
                                               accum_out=T[w][:, 0:1]), [V("p", 0, NU)], [V("junk", 0, NU), V(win, 0, 1)])
         ts(V("zz", 0, 24), V("p", 15, NU, 16), last, A.is_lt, 16.0, A.mult)
         if b == 0:
-            ts(V("q6", 0, 1), V("pd", 0, 1), 6.0, A.is_equal)
+            etile("e25", 3)
         reduce(V("h1", 0, 1), V("zz", 0, 24), A.add)
         if b == 0:
-            ts(V("cf", 0, 1), V("pd", 0, 1), 6.0, A.is_ge)
+            quant(V("r16", 0, 128), V("tr16", 0, 512))
         ts(V("mbh", 0, XL), V("mb", 0, XL), V("h1", 0, 1), A.subtract)
         ts(V("xtile", 1, 4 * XL, 4), V("mask", 0, XL), V("h1", 0, 1), A.mult, 192.0, A.min)
-        if b == 0:
-            ts(V("m6", 0, 6), V("mask", NT, XL), V("q6", 0, 1), A.subtract)
-            ts(V("pm1", 0, 1), V("pm", 0, 1), 1.0, A.add)
-            tt(V("cdig", 3, 24, 4), V("m6", 0, 6), V("iotac", 0, 6), A.mult)
-            etile("e75", 0)
         _record(rec, "scalar", "comp", lambda q: q.activation(T.xtile[:, 2:4 * XL:4], T.mb2[:, 0:XL], AF.Relu, bias=T.h1[:, 0:1]),
                 [V("mb2", 0, XL), V("h1", 0, 1)], [V("xtile", 2, 4 * XL, 4)])
-        ts(V("xtile", 0, 4 * XL, 4), V("mbh", 0, XL), V(win, 0, 1), A.add, 0.0, A.max)
-        quant(V("xl", 0, XC), V("xtile", 0, 4 * XC))
-        mm(5, V("r16", 0, 128), V("xl", 0, XC))
-        mm(6, V("r1", 0, 128), V("xl", 0, XC), True, False)
-        mm(6, V("xl", 0, XC), V("negw", 0, 128), False, True)
         if b == 0:
+            copy(V("ze", 4, 516, 4), V("ident", 0, 128), "scalar", scale=0.75)
+            for t in range(3):
+                copy(V("tr1", t, 512, 4), V("eq16", 0, 128), "scalar", scale=0.0, bias=1.0)
+            copy(V("ma", 0, 16), V("eq16", 0, 16), "scalar", scale=-1.0, bias=1.0)
+            copy(V("mc", 0, 1), V("eq16", 0, 1), "scalar", scale=0.0)
+            copy(V("mc", 1, 16), V("eq16", 0, 15), "scalar", scale=BIG)
+            copy(V("cf", 0, 1), V("pd", 0, 1), "scalar", bias=-5.0, func=AF.Relu)
+            copy(V("esc0", 0, 1), V("pm", 0, 1), "scalar", bias=-14.0, func=AF.Relu)
+            for n, c in (("nt", 4 * NT), ("mt", 0), ("xt1", 384)):
+                copy(V(n, c, c + 128), V("eq16", 0, 128), "scalar", scale=0.0)
+            copy(V("esc", 0, 1), V("esc0", 0, 1), "scalar", scale=1.0 - 1.0 / BIG, bias=1.0 / BIG)
+            ts(V("m6", 0, 6), V("mask", NT, XL), V("mask", XL, XL + 1), A.subtract)
+        ts(V("xtile", 0, 4 * XL, 4), V("mbh", 0, XL), V(win, 0, 1), A.add, 0.0, A.max)
+        if b == 0:
+            ts(V("tr1", 3, 512, 4), V("iotac", 0, 128), V("pcol", 0, 1), A.is_le, 512.0, A.mult)
+            tt(V("cdig", 3, 24, 4), V("m6", 0, 6), V("iotac", 0, 6), A.mult)
             copy(V("cdig", 0, 24, 4), V("m6", 0, 6), "scalar", scale=V("pm", 0, 1))
             copy(V("cdig", 1, 24, 4), V("m6", 0, 6), "scalar", scale=192.0)
             copy(V("cdig", 2, 24, 4), V("m6", 0, 6), "scalar", scale=192.0)
+        quant(xl, V("xtile", 0, 4 * XC))
+        for x in ("", "s"):
+            send(partner, V(ex[0] + x, 0, 6), V(xl[0] + x, NT, XL), "ae%d" % b, "le")
+        mm(5, V("r16", 0, 128), xl)
+        if b == 0:
+            etile("e75", 0)
             etile("e75", 1)
-            etile("e75", 2)
+            tokens()
         else:
             tt(V("pre", 0, 24), V("xtile", 4 * NT, 4 * XL), V("cdig", 0, 24), A.subtract)
         copy(lown, V("ps5", NT, XL))
         if b == 0:
-            send(partner, V("early", 0, 6), lown, "ae0", "ll")
+            quant(V("r1", 0, 128), V("tr1", 0, 512))
         pick(V("sel", 0, NT), V(tab, 0, NU), lown)
         if b == 0:
+            quant(V("negw", 0, 128), V("tnegw", 0, 512))
+        mm(6, V("r1", 0, 128), xl, True, False)
+        mm(6, xl, V("negw", 0, 128), False, True)
+        if b == 0:
+            etile("e75", 2)
             etile("e75", 3)
+            tt(V("mw", 0, 16), V("ma", 0, 16), V("mc", 0, 16), A.max)
             tt(V("pre", 0, 24), V("xtile", 4 * NT, 4 * XL), V("cdig", 0, 24), A.subtract)
         for t in range(4):
             mm(t, V("e75", 128 * t, 128 * t + 128), V("sel", 0, 128), False, True)
         reduce(V("dmin", 0, 1), V("ps6", 0, NT), A.min, absv=True)
-        if b == 0:
-            ts(V("esc0", 0, 1), V("pm", 0, 1), 15.0, A.is_ge, 1.0 - 1.0 / BIG, A.mult)
         ts(V("flag", 0, 1), V("dmin", 0, 1), 1.0, A.min, V("cf", 0, 1), A.max)
-        if b == 0:
-            ts(V("esc", 0, 1), V("esc0", 0, 1), 1.0 / BIG, A.add)
         ts(V("xtile", 4 * XL, 4 * XL + 24), V("pre", 0, 24), V("flag", 0, 1), A.mult)
-        if b == 0:
-            for n, c in (("nt", 4 * NT), ("mt", 0)):
-                copy(V(n, c, c + 128), V("eq16", 0, 128), "scalar", scale=0.0)
-            ts(V("ma", 0, 128), V("cmod", 0, 128), V("pm", 0, 1), A.not_equal)
-            ts(V("mc", 0, 128), V("cmod", 0, 128), V("pm1", 0, 1), A.is_equal, BIG, A.mult)
         quant(V("xf", 0, 128), V("xtile", 0, 512))
+        arrive([V(ex[0], 0, 6), V(ex[0] + "s", 0, 6)], "ae%d" % b, partner, 2)
+        mm(4, V("r16", 0, 128), ex)
         mm(7, V("r16", 0, 128), V("xf", 0, 128))
         for t in range(3):
             copy(V("nt", t, 4 * NT, 4), V("ps%d" % t, 0, NT), "scalar")
-        if b == 1:
-            copy(lx, V("ps7", XL, XL + 6))
-            send(partner, land, lx, "al1", "ll")
         copy(V("nt", 3, 4 * NT, 4), V("ps3", 0, NT))
         quant(V(tab, OWN, OWN + 128), V("nt", 0, 512))
         for x in (tab, tab + "s"):
             send(partner, V(x, PAR, PAR + NT), V(x, OWN, OWN + NT), "ac%d" % b, "lc")
-        if b == 0:
-            copy(lx, V("ps7", XL, XL + 6))
-            send(partner, land, lx, "al0", "ll")
+        copy(lx, V("ps7", XL, XL + 6))
+        send(partner, land, lx, "al%d" % b, "ll")
         store("sync", T.ch[b:b + 1, 0:NT], V(win, 0, 1), T[win][0:NT, 0:1])
         if b == 0:
-            tt(V("mw", 0, 128), V("ma", 0, 128), V("mc", 0, 128), A.max)
-            copy(V("mw", 128, 256), V("mw", 0, 128), "scalar")
-            copy(V("mw", 256, NU), V("mw", 0, 128), "scalar")
+            for c, n in ((16, 16), (32, 32), (64, 64), (128, 128), (256, 128)):
+                copy(V("mw", c, c + n), V("mw", 0, n), "scalar")
+        copy(look, V("ps4", 0, 6))
         scatter(src, lx, V("jown", 0, NT))
-        if b == 1:
-            quant(V("wq", 0, 128), V("wt", 0, 512))
-        look = land
-        if b == 0:
-            look = V("early", 0, 6)
-            arrive([look], "ae0", partner)
         arrive([land], "al%d" % b, partner)
         arrive([V(tab, PAR, PAR + NT), V(tab + "s", PAR, PAR + NT)], "ac%d" % b, partner, 2)
         copy(V("c1", 0, NT), src, off=look)
         copy(V("sg", 0, NT), src, "scalar", bias=0.5 - OWN, off=look, func=AF.Sign)
         copy(V("both", 0, NT), V("sg", 0, NT), "scalar", scale=(MRG - PAR) / 2.0)
         scan(V("c2", 0, NT), V("mw", 0, NT), V("c1", 0, NT), 0.0, A.mult, A.add)
+        if b == 0:
+            quant(V("xq1", 0, 128), V("xt1", 0, 512))
+        else:
+            quant(V("wq", 0, 128), V("wt", 0, 512))
         ts(V("clist", 0, 6), V("c2", 15, NT, 16), V("esc", 0, 1), A.mult, -0.34, A.add)
         tt(V("val", 0, NT), V("both", 0, NT), V("jpar", 0, NT), A.add)
         pick(V("selm", 32, 128), V(tab, 0, PAR), V("clist", 0, 6))
-        parts = [V(tab, PAR - 32, PAR + NT), V("selm", 0, 128)]
-        for k, x in enumerate(parts[::-1] if b == 0 else parts):
+        for k, x in enumerate((V(tab, PAR - 32, PAR + NT), V("selm", 0, 128))):
             for t in range(4):
                 mm(t, V("e25", 128 * t, 128 * t + 128), x, k == 0, k == 1)
         scatter(src, land, V("val", 0, NT))
         scan(V("srcs", 0, NU), V("mw", 0, NU), V(src[0], 0, NU), 0.0, A.mult, A.add)
         ts(V("blist", 0, 24), V("srcs", 15, NU, 16), V("esc", 0, 1), A.mult, -0.34, A.add)
-        if b == 0:
-            memset(V("xt1", 384, 512), 0.0)
-            quant(V("xq1", 0, 128), V("xt1", 0, 512))
         for t in range(4):
             copy(V("mt", 128 + t, 512, 4), V("ps%d" % t, 32, 128), "scalar", scale=2.0)
         quant(V(tab, MQ, MQ + 128), V("mt", 0, 512))
@@ -438,6 +442,7 @@ def rank_program(g, core, T, topo):
         store("scalar", T.osc[4 * k:4 * k + 4, 0:NU], V("fins", 0, NU), T.fins[32 * k:32 * k + 4, 0:NU])
     _record(rec, "sync", "end", None, [], [], stores)
     _issue(rec, {"vector": g.vector, "scalar": g.scalar, "tensor": g.tensor, "gpsimd": g, "sync": g.sync}, T.sem)
-    n = [len(lanes(core, T.cores[rank ^ (1 << b)])) for b in range(NR)]
-    g.wait_ge(T.sem.ll, 2 * n[0] + n[1])
-    g.wait_ge(T.sem.lc, 2 * n[0] + 2 * n[1])
+    n = sum(len(lanes(core, T.cores[rank ^ (1 << b)])) for b in range(NR))
+    g.wait_ge(T.sem.ll, n)
+    g.wait_ge(T.sem.le, 2 * n)
+    g.wait_ge(T.sem.lc, 2 * n)

from concourse.mybir import dt, AluOpType, AxisListType, ActivationFunctionType

A = AluOpType
AF = ActivationFunctionType
NU, NT, NR = 384, 96, 2
OWN, PAR, MRG, WIN = 384, 512, 640, 736
MQ = 608
XC, XL = 128, 102
BIG = 16384.0
PIECES = ((4, 0, 128), (5, 128, 256), (6, 256, NU))
F4, F32, BF, U16, I32, U8 = "float8_e4m3fn_x4", "float32", "bfloat16", "uint16", "int32", "uint8"


def _decl():
    s = {}

    def add(n, w, t, where="sbuf"):
        s[n] = (where, [128, w], t)

    def pair(n, w):
        add(n, w, F4)
        add(n + "s", w, U8)
    for b in range(NR):
        pair("tab%d" % b, WIN)
        pair("xq%d" % b, 128)
        pair("xl%d" % b, 128)
        pair("ex%d" % b, 128)
        add("xt%d" % b, 512, BF)
        for n in ("lown", "lx", "land", "look"):
            add("%s%d" % (n, b), 6, U16)
        add("src%d" % b, 480, F32)
        add("win%d" % b, 1, F32)
    for n in ("e25", "e75"):
        pair(n, 512)
    for n in ("r16", "r1", "negw"):
        pair(n, 128)
        add("t" + n, 512, BF)
    for n in ("sel", "selm", "xf", "wq"):
        pair(n, 128)
    pair("fin", NU)
    for n in range(8):
        add("ps%d" % n, 512, F32, "psum")
    for n, w, t in (("kbt", 1536, BF), ("wt", 512, BF), ("nt", 512, BF), ("mt", 512, BF), ("xtile", 4 * XC, BF), ("ones", 128, BF),
                    ("ident", 128, BF), ("ze", 520, BF), ("mask", XL + 1, BF), ("junk", NU, BF), ("mb", XL, BF), ("mbh", XL, BF),
                    ("mb2", XL, BF), ("negc", 128, BF), ("cmod", 128, BF), ("iotac", 128, BF), ("eq16", 128, BF), ("ma", 16, BF),
                    ("mc", 16, BF), ("mw", NU, BF), ("m6", 6, BF), ("cdig", 24, BF), ("pre", 24, BF),
                    ("ip", 1, I32), ("pmi", 1, I32), ("pdi", 1, I32), ("clist", 6, U16), ("blist", 24, U16)):
        add(n, w, t)
    for n, w in (("jown", NT), ("jpar", NT), ("pcol", 1), ("pm", 1), ("pd", 1), ("p", NU), ("zz", 24), ("h1", 1),
                 ("dmin", 1), ("flag", 1), ("cf", 1), ("esc0", 1), ("esc", 1), ("c1", NT), ("c2", NT), ("sg", NT),
                 ("both", NT), ("val", NT), ("srcs", NU), ("ysb", NU)):
        add(n, w, F32)
    return s


SCRATCH = _decl()
NCOMP, NHW = 90, 30
REMOTE = ["%s%d" % (n, b) for b in range(NR) for n in ("ae", "al", "ac")] + ["le", "ll", "lc"]
SEMAPHORES = ["c%d" % i for i in range(NCOMP)] + ["h%d" % i for i in range(NHW)] + REMOTE


def _clash(u, v):
    if u[1] >= v[2] or v[1] >= u[2]:
        return False
    return not (u[3] == v[3] and u[3] > 1 and (u[1] - v[1]) % u[3])


def _record(rec, queue, kind, call, reads, writes, extra=()):
    ops, acc = rec["ops"], rec["acc"]
    i = len(ops)
    deps = set(extra)
    for vs, w in ((reads, False), (writes, True)):
        for v in vs:
            for (u, uw, j, uq) in acc.get(v[0], []):
                if v[0] in rec["psum"]:
                    if uq == "tensor" and queue == "tensor":
                        continue
                    if uq != queue or uw:
                        deps.add(j)
                elif (w or uw) and _clash(u, v):
                    deps.add(j)
    for vs, w in ((reads, False), (writes, True)):
        for v in vs:
            acc.setdefault(v[0], []).append((v, w, i, queue))
    if kind == "arr" and deps:
        raise ValueError("a landing buffer is in use")
    known = rec["known"].setdefault(queue, set()) if kind != "arr" else set()
    waits = []
    for j in sorted(deps, reverse=True):
        if j not in known:
            waits.append(j)
            known.add(j)
            known |= ops[j]["known"]
    ops.append({"queue": queue, "kind": kind, "call": call, "waits": waits, "known": set(known), "need": False})
    for j in waits:
        ops[j]["need"] = True
    return i


def _issue(rec, queues, sems):
    ops = rec["ops"]
    last, total = {}, {}
    for i, o in enumerate(ops):
        if o["kind"] == "arr":
            o["sem"], o["val"] = o["call"]
            continue
        q = queues[o["queue"]]
        for j in reversed(o["waits"]):
            q.wait_ge(sems[ops[j]["sem"]], ops[j]["val"])
        if o["kind"] == "end":
            continue
        ins = o["call"](q)
        if not o["need"] or o["kind"] == "remote":
            continue
        pool = ["h%d" % k for k in range(NHW)] if o["kind"] == "dma" else ["c%d" % k for k in range(NCOMP)]
        name = None
        for s in pool:
            if s not in last or last[s] in o["known"]:
                name = s
                break
        if name is None:
            raise ValueError("out of semaphores")
        n = 16 if o["kind"] == "dma" else 1
        ins.then_inc(sems[name], n)
        last[name] = i
        total[name] = total.get(name, 0) + n
        o["sem"], o["val"] = name, total[name]


def V(name, a, b, s=1):
    return (name, a, b, s)


def rank_program(g, core, T, topo):
    rank = T.rank_of(core)
    if rank is None:
        return
    rec = {"ops": [], "acc": {}, "known": {}, "psum": ["ps%d" % n for n in range(8)]}

    def ap(v):
        return T[v[0]][:, v[1]:v[2]] if v[3] == 1 else T[v[0]][:, v[1]:v[2]:v[3]]

    def sc(v):
        return (v[0] + "s", v[1], v[2], 1)

    def views(*xs):
        return [x for x in xs if isinstance(x, tuple)]

    def val(x):
        return ap(x) if isinstance(x, tuple) else x

    def lanes(src, dst):
        return topo.engines(src, dst)[::2]

    def memset(out, c):
        _record(rec, "vector", "comp", lambda q: q.memset(ap(out), c), [], [out])

    def copy(out, in_, queue="vector", scale=None, bias=None, off=None, func=None):
        src = (lambda: ap(in_)) if off is None else (lambda: ap(in_).indirect(ap(off)))
        if queue == "vector":
            _record(rec, "vector", "comp", lambda q: q.tensor_copy(ap(out), src()), views(in_, off), [out])
            return
        f = func or (AF.Copy if bias is None else AF.Identity)
        kw = {}
        if scale is not None:
            kw["scale"] = val(scale)
        if bias is not None:
            kw["bias"] = bias
        _record(rec, "scalar", "comp", lambda q: q.activation(ap(out), src(), f, **kw), views(in_, scale, off), [out])

    def ts(out, in0, s1, op0, s2=None, op1=None):
        def call(q):
            if op1 is None:
                return q.tensor_scalar(ap(out), ap(in0), val(s1), None, op0)
            return q.tensor_scalar(ap(out), ap(in0), val(s1), val(s2), op0, op1)
        _record(rec, "vector", "comp", call, views(in0, s1, s2), [out])

    def tt(out, in0, in1, op):
        _record(rec, "vector", "comp", lambda q: q.tensor_tensor(ap(out), ap(in0), ap(in1), op), [in0, in1], [out])

    def scatter(win, off, in_):
        _record(rec, "vector", "comp", lambda q: q.tensor_copy(ap(win).indirect(ap(off)), ap(in_)), [win, off, in_], [win])

    def reduce(out, in_, op, absv=False):
        def call(q):
            if absv:
                return q.tensor_reduce(ap(out), ap(in_), AxisListType.X, op, apply_absolute_value=True)
            return q.tensor_reduce(ap(out), ap(in_), AxisListType.X, op)
        _record(rec, "vector", "comp", call, [in_], [out])

    def scan(out, d0, d1, init, op0, op1):
        _record(rec, "vector", "comp", lambda q: q.tensor_tensor_scan(ap(out), ap(d0), ap(d1), val(init), op0, op1),
                views(d0, d1, init), [out])

    def quant(out, in_):
        _record(rec, "vector", "comp", lambda q: q.quantize_mx(ap(out), ap(sc(out)), ap(in_)), [in_], [out, sc(out)])

    def mm(ps, w, x, start=True, stop=True):
        n = x[2] - x[1]
        _record(rec, "tensor", "comp",
                lambda q: q.matmul_mx(T["ps%d" % ps][:, 0:n], ap(w), ap(sc(w)), ap(x), ap(sc(x)), start, stop),
                [w, sc(w), x, sc(x)], [V("ps%d" % ps, 0, n)])

    def pick(out, win, off):
        _record(rec, "vector", "comp",
                lambda q: q.tensor_copy(ap(out).bitcast(dt.uint32), ap(win).bitcast(dt.uint32).indirect(ap(off))), [win, off], [out])
        _record(rec, "scalar", "comp", lambda q: q.activation(ap(sc(out)), ap(sc(win)).indirect(ap(off)), AF.Copy),
                [sc(win), off], [sc(out)])

    def iota(out, pattern, base, cm):
        f = SCRATCH[out[0]][2] != I32

        def call(q):
            if f:
                return q.iota(ap(out), pattern, base, cm, allow_small_or_imprecise_dtypes=True)
            return q.iota(ap(out), pattern, base, cm)
        _record(rec, "gpsimd", "comp", call, [], [out])

    def load(queue, out, src, after=()):
        return _record(rec, queue, "dma", lambda q: q.dma_start(ap(out), src), [], [out], after)

    def lay(out, in_):
        _record(rec, "sync", "dma", lambda q: q.dma_start(ap(out).bitcast(dt.uint8), ap(in_).bitcast(dt.uint8)), [in_], [out])
        _record(rec, "sync", "dma", lambda q: q.dma_start(ap(sc(out)), ap(sc(in_))), [sc(in_)], [sc(out)])

    stores = []

    def store(queue, dst, in_, view):
        stores.append(_record(rec, queue, "dma", lambda q: q.dma_start(dst, view), [in_], []))

    def send(dst, out, in_, arr, loc):
        rid, pid, _s = topo.addr(dst)
        codes = SCRATCH[in_[0]][2] == F4

        def call(q):
            o, i = ap(out), ap(in_)
            if codes:
                o, i = o.bitcast(dt.uint8), i.bitcast(dt.uint8)
            return q.remote_dma(o, i, T.sem[arr], T.sem[loc], pid, rid, sum(1 << e for e in lanes(core, dst)))
        _record(rec, "gpsimd", "remote", call, [in_], [])

    def arrive(writes, sem, src, calls=1):
        _record(rec, "network", "arr", (sem, calls * len(lanes(src, core))), [], writes)

    load("sync", V("xt0", 0, 384), T.x[:, 0:384])
    load("scalar", V("kbt", 0, 512), T.kb[:, 0:512])
    load("sync", V("kbt", 512, 1024), T.kb[:, 512:1024])
    kb2 = load("sync", V("kbt", 1024, 1536), T.kb[:, 1024:1536])

    iota(V("ip", 0, 1), [[0, 1]], 0, 1)
    memset(V("ones", 0, 128), 1.0)
    _record(rec, "gpsimd", "comp", lambda q: q.affine_select(T.ident[:, 0:128], T.ones[:, 0:128], [[-1, 128]], A.is_equal, 0.0, 0, 1),
            [V("ones", 0, 128)], [V("ident", 0, 128)])
    iota(V("cmod", 0, 128), [[0, 8], [1, 16]], 0, 0)
    iota(V("pcol", 0, 1), [[0, 1]], 0, 1)
    iota(V("iotac", 0, 128), [[1, 128]], 0, 0)
    iota(V("jown", 0, NT), [[1, NT]], OWN, 0)
    iota(V("src0", 0, 480), [[1, 480]], 0, 0)
    iota(V("jpar", 0, NT), [[1, NT]], (PAR + MRG) // 2, 0)
    iota(V("src1", 0, 480), [[1, 480]], 0, 0)
    memset(V("ze", 0, 520), 0.0)
    copy(V("ze", 4, 516, 4), V("ident", 0, 128), "scalar", scale=0.25)
    memset(V("xt0", 384, 512), 0.0)
    memset(V("negc", 0, 128), -1e29)
    ts(V("pmi", 0, 1), V("ip", 0, 1), 15, A.bitwise_and)
    ts(V("pdi", 0, 1), V("ip", 0, 1), 4, A.logical_shift_right)
    memset(V("xtile", 4 * XL, 4 * XC), 0.0)
    copy(V("pm", 0, 1), V("pmi", 0, 1))
    copy(V("pd", 0, 1), V("pdi", 0, 1))
    memset(V("xtile", 4 * NT + 3, 4 * XL, 4), 0.0)
    copy(V("xtile", 3, 4 * NT, 4), V("ident", 0, NT), "scalar")
    copy(V("mask", 0, NT), V("ident", 0, NT), "scalar")

    def etile(n, t):
        quant(V(n, 128 * t, 128 * t + 128), V("ze", 4 - t, 516 - t))

    def score(b, ps, u, v):
        mm(ps, V("xq%d" % b, 0, 128), V("tab%d" % b, u, v))

    def run_max(ps, u, v):
        scan(V("p", u, v), V("ps%d" % ps, 0, v - u), V("negc", 0, v - u), V("p", u - 1, u) if u else -1e29, A.max, A.max)

    def units(ps, u, v):
        quant(V("tab0", u, v), V("kbt", 4 * u, 4 * v))
        score(0, ps, u, v)

    quant(V("xq0", 0, 128), V("xt0", 0, 512))
    lay(V("sel", 96, 128), V("xq0", 96, 128))
    lay(V("selm", 0, 32), V("xq0", 96, 128))
    for b in range(NR):
        lay(V("ex%d" % b, 6, 128), V("xq0", 0, 122))
    load("sync", V("xt1", 0, 384), T.x[:, 384:768], [kb2])
    load("sync", V("wt", 0, 512), T.w[:, 0:512], [kb2])
    etile("e25", 0)
    units(*PIECES[0])
    etile("e25", 1)
    units(*PIECES[1])
    ts(V("eq16", 0, 128), V("cmod", 0, 128), V("pm", 0, 1), A.is_equal)
    for t in range(4):
        copy(V("tr16", t, 512, 4), V("eq16", 0, 128), "scalar", scale=16.0 if t == 3 else 1.0)
    run_max(*PIECES[0])
    units(*PIECES[2])
    ts(V("mask", NT, XL + 1), V("iotac", 0, 7), V("pd", 0, 1), A.is_equal)
    copy(V("mb", 0, XL), V("mask", 0, XL), "scalar", scale=1024.0, bias=-1024.0)
    copy(V("mb2", 0, XL), V("mask", 0, XL), "scalar", scale=1024.0, bias=-1024.0 - 192.0)
    run_max(*PIECES[1])
    memset(V("tnegw", 0, 512), -1.0)
    run_max(*PIECES[2])
    memset(V("tnegw", 3, 512, 4), 0.0)
    etile("e25", 2)

    for b in range(NR):
        tab, xq, nxt = "tab%d" % b, "xq%d" % b, "tab%d" % (b + 1) if b + 1 < NR else "fin"
        win, src = "win%d" % b, V("src%d" % b, 0, 480)
        lown, lx, land, look = [V("%s%d" % (n, b), 0, 6) for n in ("lown", "lx", "land", "look")]
        xl, ex = V("xl%d" % b, 0, XC), V("ex%d" % b, 0, 128)
        partner = T.cores[rank ^ (1 << b)]

        def tokens(xq=xq):
            for t in range(4):
                mm(t, V("e25", 128 * t, 128 * t + 128), V(xq, 0, 128), True, False)

        if b == 1:
            tokens()
        last = V("p", NU - 1, NU)
        _record(rec, "scalar", "comp",
                lambda q, w=win: q.activation(T.junk[:, 0:NU], T.p[:, 0:NU], AF.Sign, bias=T.p[:, NU - 1:NU], scale=-1.0,
                                              accum_out=T[w][:, 0:1]), [V("p", 0, NU)], [V("junk", 0, NU), V(win, 0, 1)])
        ts(V("zz", 0, 24), V("p", 15, NU, 16), last, A.is_lt, 16.0, A.mult)
        if b == 0:
            etile("e25", 3)
        reduce(V("h1", 0, 1), V("zz", 0, 24), A.add)
        if b == 0:
            quant(V("r16", 0, 128), V("tr16", 0, 512))
        ts(V("mbh", 0, XL), V("mb", 0, XL), V("h1", 0, 1), A.subtract)
        ts(V("xtile", 1, 4 * XL, 4), V("mask", 0, XL), V("h1", 0, 1), A.mult, 192.0, A.min)
        _record(rec, "scalar", "comp", lambda q: q.activation(T.xtile[:, 2:4 * XL:4], T.mb2[:, 0:XL], AF.Relu, bias=T.h1[:, 0:1]),
                [V("mb2", 0, XL), V("h1", 0, 1)], [V("xtile", 2, 4 * XL, 4)])
        if b == 0:
            copy(V("ze", 4, 516, 4), V("ident", 0, 128), "scalar", scale=0.75)
            for t in range(3):
                copy(V("tr1", t, 512, 4), V("eq16", 0, 128), "scalar", scale=0.0, bias=1.0)
            copy(V("ma", 0, 16), V("eq16", 0, 16), "scalar", scale=-1.0, bias=1.0)
            copy(V("mc", 0, 1), V("eq16", 0, 1), "scalar", scale=0.0)
            copy(V("mc", 1, 16), V("eq16", 0, 15), "scalar", scale=BIG)
            copy(V("cf", 0, 1), V("pd", 0, 1), "scalar", bias=-5.0, func=AF.Relu)
            copy(V("esc0", 0, 1), V("pm", 0, 1), "scalar", bias=-14.0, func=AF.Relu)
            for n, c in (("nt", 4 * NT), ("mt", 0), ("xt1", 384)):
                copy(V(n, c, c + 128), V("eq16", 0, 128), "scalar", scale=0.0)
            copy(V("esc", 0, 1), V("esc0", 0, 1), "scalar", scale=1.0 - 1.0 / BIG, bias=1.0 / BIG)
            ts(V("m6", 0, 6), V("mask", NT, XL), V("mask", XL, XL + 1), A.subtract)
        ts(V("xtile", 0, 4 * XL, 4), V("mbh", 0, XL), V(win, 0, 1), A.add, 0.0, A.max)
        if b == 0:
            ts(V("tr1", 3, 512, 4), V("iotac", 0, 128), V("pcol", 0, 1), A.is_le, 512.0, A.mult)
            tt(V("cdig", 3, 24, 4), V("m6", 0, 6), V("iotac", 0, 6), A.mult)
            copy(V("cdig", 0, 24, 4), V("m6", 0, 6), "scalar", scale=V("pm", 0, 1))
            copy(V("cdig", 1, 24, 4), V("m6", 0, 6), "scalar", scale=192.0)
            copy(V("cdig", 2, 24, 4), V("m6", 0, 6), "scalar", scale=192.0)
        quant(xl, V("xtile", 0, 4 * XC))
        for x in ("", "s"):
            send(partner, V(ex[0] + x, 0, 6), V(xl[0] + x, NT, XL), "ae%d" % b, "le")
        mm(5, V("r16", 0, 128), xl)
        if b == 0:
            etile("e75", 0)
            etile("e75", 1)
            tokens()
        else:
            tt(V("pre", 0, 24), V("xtile", 4 * NT, 4 * XL), V("cdig", 0, 24), A.subtract)
        copy(lown, V("ps5", NT, XL))
        if b == 0:
            quant(V("r1", 0, 128), V("tr1", 0, 512))
        pick(V("sel", 0, NT), V(tab, 0, NU), lown)
        if b == 0:
            quant(V("negw", 0, 128), V("tnegw", 0, 512))
        mm(6, V("r1", 0, 128), xl, True, False)
        mm(6, xl, V("negw", 0, 128), False, True)
        if b == 0:
            etile("e75", 2)
            etile("e75", 3)
            tt(V("mw", 0, 16), V("ma", 0, 16), V("mc", 0, 16), A.max)
            tt(V("pre", 0, 24), V("xtile", 4 * NT, 4 * XL), V("cdig", 0, 24), A.subtract)
        for t in range(4):
            mm(t, V("e75", 128 * t, 128 * t + 128), V("sel", 0, 128), False, True)
        reduce(V("dmin", 0, 1), V("ps6", 0, NT), A.min, absv=True)
        ts(V("flag", 0, 1), V("dmin", 0, 1), 1.0, A.min, V("cf", 0, 1), A.max)
        ts(V("xtile", 4 * XL, 4 * XL + 24), V("pre", 0, 24), V("flag", 0, 1), A.mult)
        quant(V("xf", 0, 128), V("xtile", 0, 512))
        arrive([V(ex[0], 0, 6), V(ex[0] + "s", 0, 6)], "ae%d" % b, partner, 2)
        mm(4, V("r16", 0, 128), ex)
        mm(7, V("r16", 0, 128), V("xf", 0, 128))
        for t in range(3):
            copy(V("nt", t, 4 * NT, 4), V("ps%d" % t, 0, NT), "scalar")
        copy(V("nt", 3, 4 * NT, 4), V("ps3", 0, NT))
        quant(V(tab, OWN, OWN + 128), V("nt", 0, 512))
        for x in (tab, tab + "s"):
            send(partner, V(x, PAR, PAR + NT), V(x, OWN, OWN + NT), "ac%d" % b, "lc")
        copy(lx, V("ps7", XL, XL + 6))
        send(partner, land, lx, "al%d" % b, "ll")
        store("sync", T.ch[b:b + 1, 0:NT], V(win, 0, 1), T[win][0:NT, 0:1])
        if b == 0:
            for c, n in ((16, 16), (32, 32), (64, 64), (128, 128), (256, 128)):
                copy(V("mw", c, c + n), V("mw", 0, n), "scalar")
        copy(look, V("ps4", 0, 6))
        scatter(src, lx, V("jown", 0, NT))
        arrive([land], "al%d" % b, partner)
        arrive([V(tab, PAR, PAR + NT), V(tab + "s", PAR, PAR + NT)], "ac%d" % b, partner, 2)
        copy(V("c1", 0, NT), src, off=look)
        copy(V("sg", 0, NT), src, "scalar", bias=0.5 - OWN, off=look, func=AF.Sign)
        copy(V("both", 0, NT), V("sg", 0, NT), "scalar", scale=(MRG - PAR) / 2.0)
        scan(V("c2", 0, NT), V("mw", 0, NT), V("c1", 0, NT), 0.0, A.mult, A.add)
        if b == 0:
            quant(V("xq1", 0, 128), V("xt1", 0, 512))
        else:
            quant(V("wq", 0, 128), V("wt", 0, 512))
        ts(V("clist", 0, 6), V("c2", 15, NT, 16), V("esc", 0, 1), A.mult, -0.34, A.add)
        tt(V("val", 0, NT), V("both", 0, NT), V("jpar", 0, NT), A.add)
        pick(V("selm", 32, 128), V(tab, 0, PAR), V("clist", 0, 6))
        for k, x in enumerate((V(tab, PAR - 32, PAR + NT), V("selm", 0, 128))):
            for t in range(4):
                mm(t, V("e25", 128 * t, 128 * t + 128), x, k == 0, k == 1)
        scatter(src, land, V("val", 0, NT))
        scan(V("srcs", 0, NU), V("mw", 0, NU), V(src[0], 0, NU), 0.0, A.mult, A.add)
        ts(V("blist", 0, 24), V("srcs", 15, NU, 16), V("esc", 0, 1), A.mult, -0.34, A.add)
        for t in range(4):
            copy(V("mt", 128 + t, 512, 4), V("ps%d" % t, 32, 128), "scalar", scale=2.0)
        quant(V(tab, MQ, MQ + 128), V("mt", 0, 512))
        for ps, u, v in PIECES:
            pick(V(nxt, u, v), V(tab, 0, WIN), V("blist", u // 16, v // 16))
            if b + 1 < NR:
                score(b + 1, ps, u, v)
        if b + 1 < NR:
            for piece in PIECES:
                run_max(*piece)

    for ps, u, v in PIECES:
        mm(ps, V("wq", 0, 128), V("fin", u, v))
        store("sync", T.oc[:, 4 * u:4 * v], V("fin", u, v), T.fin[:, u:v].bitcast(dt.uint8))
    for ps, u, v in PIECES:
        copy(V("ysb", u, v), V("ps%d" % ps, 0, v - u), "scalar" if u == 128 else "vector")
        store("sync", T.y[:, u:v], V("ysb", u, v), T.ysb[:, u:v])
    for k in range(4):
        store("scalar", T.osc[4 * k:4 * k + 4, 0:NU], V("fins", 0, NU), T.fins[32 * k:32 * k + 4, 0:NU])
    _record(rec, "sync", "end", None, [], [], stores)
    _issue(rec, {"vector": g.vector, "scalar": g.scalar, "tensor": g.tensor, "gpsimd": g, "sync": g.sync}, T.sem)
    n = sum(len(lanes(core, T.cores[rank ^ (1 << b)])) for b in range(NR))
    g.wait_ge(T.sem.ll, n)
    g.wait_ge(T.sem.le, 2 * n)
    g.wait_ge(T.sem.lc, 2 * n)
